import numpy as np
import ml_dtypes


def mxq(x, axis, fmt="e4m3"):
    dtype, down = {"e4m3": (ml_dtypes.float8_e4m3fn, 7), "e5m2": (ml_dtypes.float8_e5m2, 14)}[fmt]
    v = np.moveaxis(np.asarray(x, np.float32).astype(ml_dtypes.bfloat16).astype(np.float64), axis, -1)
    blocks = v.reshape(v.shape[:-1] + (-1, 32))
    amax = np.abs(blocks).max(-1, keepdims=True)
    byte = np.maximum(np.where(amax > 0, np.frexp(amax)[1] - 1 + 127, 0) - down, 1)
    scale = np.exp2(byte - 127.0)
    codes = (blocks / scale).astype(np.float32).astype(dtype).astype(np.float64)
    return np.moveaxis((codes * scale).reshape(v.shape), -1, axis)


WIDE = False


def mx_kscale(k):
    if not WIDE:
        return np.ones(k)
    levels = np.array([10, -10, 5, -5, 0])
    if k % 512:
        return np.exp2(np.random.permutation(np.resize(levels, k // 32))).repeat(32)
    a = np.empty((k // 512, 16))
    for p in range(k // 512):
        a[p, :8] = np.random.permutation(np.resize(levels, 8))
        for g in range(8):
            far = levels[np.abs(levels - a[p, g]) >= 10]
            a[p, g + 8] = far[np.random.randint(len(far))]
    return np.exp2(a.ravel()).repeat(32)


def f64(x):
    return np.asarray(x).astype(np.float64)


def striped(idx):
    return np.tile(idx.reshape(-1, 16).T, (8, 1)).astype(np.uint16)


def unstriped(offs):
    return offs[:16].T.reshape(-1).astype(np.int64)


def relu(v):
    return np.maximum(v, 0.0)


K, T, S, H, N = 512, 1024, 512, 1024, 512


def setup_inputs():
    n = np.random.standard_normal
    s = mx_kscale(K)[:, None]
    u = mx_kscale(H)
    return {
        "xT": (n((K, T)) * s).astype(np.float32),
        "w1": (n((K, H)) / np.sqrt(K) / s).astype(np.float32),
        "w3": (n((K, H)) / np.sqrt(K) / s * u).astype(np.float32),
        "w2": (n((H, N)) / np.sqrt(H) / u[:, None]).astype(np.float32),
        "offs": striped(np.sort(np.random.permutation(T)[:S])),
    }


def reference(xT, w1, w3, w2, offs):
    idx = unstriped(offs)
    xq = mxq(f64(xT)[:, idx], 0, "e4m3")
    h = relu(mxq(f64(w1), 0, "e4m3").T @ xq) * (mxq(f64(w3), 0, "e4m3").T @ xq)
    y = mxq(f64(w2), 0, "e4m3").T @ mxq(h, 0, "e4m3")
    return y

@@ -1,0 +1,216 @@
+from contextlib import ExitStack
+
+import concourse.mybir as mybir
+
+K, T, S, H, N = 512, 1024, 512, 1024, 512
+FLOPS = 2 * S * (2 * K * H + H * N)
+
+F32 = mybir.dt.float32
+BF16 = mybir.dt.bfloat16
+U32 = mybir.dt.uint32
+U16 = mybir.dt.uint16
+U8 = mybir.dt.uint8
+FP8X4 = mybir.dt.float8_e4m3fn_x4
+ADD = mybir.AluOpType.add
+MULT = mybir.AluOpType.mult
+RELU = mybir.ActivationFunctionType.Relu
+
+P = 128
+J = 4
+KP = P * J
+NB = 128
+Q = 256
+
+ORDER = [["x",0,512],["x",512,512],["a",0,512],["b",0,512],["a",512,512],["b",512,256],["b",768,256],["c",0,512],["d",0,256],["d",256,256]]
+SPLIT = {"x0":[["V",160],["S",96]],"x256":[["V",128],["S",128]],"x512":[["S",256]],"x768":[["V",256]],"a0":[["V",160],["S",96]],"a256":[["S",256]],"b0":[["V",192],["S",64]],"b256":[["S",256]],"a512":[["V",256]],"a768":[["V",224],["S",32]],"b512":[["V",64],["S",192]],"b768":[["S",256]],"c0":[["S",256]],"c256":[["V",96],["S",32]],"c384":[["S",128]],"d0":[["S",256]],"d256":[["S",128]],"d384":[["V",128]]}
+STAGES = ["d0","b1","a0","c0","b0","x","a1","h0","h1","c1","d1","d2","c2"]
+H_GROUP = [4,2]
+X_QUANT = [[0,512],[512,256],[768,256]]
+W2_QUANT = [[0,256],[256,128],[384,128]]
+L2 = [[[0,1,2,"S"]],[[1,0,2,"S"]],[[1,1,2,"V"]],[[0,0,2,"S"]],[[2,0,2,"S"]],[[2,1,2,"V"]],[[3,0,2,"V"]],[[3,1,2,"S"]]]
+G_STEP = 256
+
+
+def tile_picked_pick_glu_relu_srt_e_kernel(tc, xT, w1, w3, w2, offs, out):
+    nc = tc.nc
+
+    def copy(engine, dst, src):
+        if engine == "V":
+            nc.vector.tensor_copy(out=dst, in_=src)
+        elif engine == "S":
+            nc.scalar.copy(out=dst, in_=src)
+        else:
+            nc.gpsimd.tensor_scalar(out=dst, in0=src, scalar1=1.0, scalar2=0.0, op0=MULT, op1=ADD)
+
+    with ExitStack() as ctx:
+        keep = ctx.enter_context(tc.tile_pool(name="keep", bufs=1))
+        psum = ctx.enter_context(tc.psum_pool(name="psum", bufs=8))
+
+        offsets = keep.tile([P, S // 16], U16, name="offsets")
+        sources = {
+            "x": xT.rearrange("(p j) w -> p j w", j=J),
+            "a": w1.rearrange("(p j) w -> p j w", j=J),
+            "b": w3.rearrange("(p j) w -> p j w", j=J),
+            "c": w2[:KP, :].rearrange("(p j) w -> p j w", j=J),
+            "d": w2[KP:, :].rearrange("(p j) w -> p j w", j=J),
+        }
+        raws = {}
+        for i, (key, first, width) in enumerate(ORDER):
+            raw = keep.tile([P, J, width], F32, name=f"raw_{key}_{first}")
+            nc.sync.dma_start(out=raw[:], in_=sources[key][:, :, first : first + width])
+            for sub in range(0, width, 128):
+                raws[(key, first + sub)] = (raw, sub)
+            if i == 0:
+                nc.sync.dma_start(offsets[:], offs)
+
+        x_codes = keep.tile([P, T], U32, name="x_codes", align_bytes=64)
+        x_scales = keep.tile([P, T], U8, name="x_scales", align_bytes=64)
+        nc.gpsimd.memset(x_scales[:], 0)
+        xg_codes = keep.tile([P, S], U32, name="xg_codes", align_bytes=64)
+        xg_scales = keep.tile([P, S], U8, name="xg_scales", align_bytes=64)
+
+        def shares(key, first):
+            found = []
+            a = 0
+            for engine, n in SPLIT[f"{key}{first}"]:
+                step = G_STEP if engine == "G" else n
+                for s in range(0, n, step):
+                    found.append((engine, a + s, a + min(s + step, n)))
+                a += n
+            return found
+
+        def plain_casts(key, first, grouped):
+            for engine, a, b in shares(key, first):
+                raw, sub = raws[(key, first)]
+                copy(
+                    engine,
+                    grouped[:, a:b, :].rearrange("p (c i) j -> p c j i", i=4),
+                    raw[:, :, sub + a : sub + b].rearrange("p j (c i) -> p c j i", i=4),
+                )
+
+        def tokens():
+            for first, width in X_QUANT:
+                grouped = keep.tile([P, width, J], BF16, name=f"x_grouped{first}", align_bytes=64)
+                for sub in range(0, width, Q):
+                    plain_casts("x", first + sub, grouped[:, sub : sub + Q, :])
+                nc.vector.quantize_mx(
+                    out=x_codes[:, first : first + width].bitcast(FP8X4),
+                    scales=x_scales[:, first : first + width],
+                    in_=grouped[:].rearrange("p w j -> p (w j)"),
+                )
+            nc.vector.tensor_copy(xg_codes[:], x_codes[:].indirect(offsets[:]))
+            nc.vector.tensor_copy(xg_scales[:], x_scales[:].indirect(offsets[:]))
+
+        w_codes = {}
+        w_scales = {}
+
+        def first_weights(w, c):
+            grouped = keep.tile([P, J, P, J], BF16, name=f"w_grouped_{w}{c}", align_bytes=64)
+            codes = keep.tile([P, KP], U32, name=f"w_codes_{w}{c}", align_bytes=64)
+            scales = keep.tile([P, KP], U8, name=f"w_scales_{w}{c}", align_bytes=64)
+            for sub in (0, Q):
+                raw, at = raws[(w, c * KP + sub)]
+                m0 = sub // 4
+                for engine, a, b in shares(w, c * KP + sub):
+                    copy(
+                        engine,
+                        grouped[:, :, m0 + a // 4 : m0 + b // 4, :].rearrange("p t m j -> p m t j"),
+                        raw[:, :, at + a : at + b].rearrange("p j (m t) -> p m t j", t=4),
+                    )
+            nc.vector.quantize_mx(
+                out=codes[:].bitcast(FP8X4), scales=scales[:], in_=grouped[:].rearrange("p t m j -> p (t m j)")
+            )
+            w_codes[(w, c)] = codes
+            w_scales[(w, c)] = scales
+
+        h_codes = {}
+        h_scales = {}
+
+        def products(w, c, b):
+            cols = slice(b * NB, (b + 1) * NB)
+            bank = psum.tile([P, J, NB], F32, name="bank", tag="bank")
+            for t in range(J):
+                rows = slice(t * P, (t + 1) * P)
+                nc.tensor.matmul_mx(
+                    out=bank[:, t, :],
+                    lhsT=w_codes[(w, c)][:, rows].bitcast(FP8X4),
+                    lhsT_scale=w_scales[(w, c)][:, rows],
+                    rhs=xg_codes[:, cols].bitcast(FP8X4),
+                    rhs_scale=xg_scales[:, cols],
+                    start=True,
+                    stop=True,
+                )
+            return bank[:].rearrange("p t n -> p n t")
+
+        def first_layer(c):
+            grouped = keep.tile([P, S, J], BF16, name=f"h_grouped{c}", align_bytes=64)
+            codes = keep.tile([P, S], U32, name=f"h_codes{c}", align_bytes=64)
+            scales = keep.tile([P, S], U8, name=f"h_scales{c}", align_bytes=64)
+            gates = []
+            for b in range(S // NB):
+                gate = keep.tile([P, NB, J], F32, name=f"gate{c}_{b}")
+                nc.scalar.activation(gate[:], products("a", c, b), RELU)
+                gates.append(gate)
+            for b in range(S // NB):
+                up = products("b", c, b)
+                nc.vector.tensor_tensor(
+                    out=grouped[:, b * NB : (b + 1) * NB, :], in0=gates[b][:], in1=up, op=MULT
+                )
+                if (b + 1) % H_GROUP[c] == 0:
+                    cols = slice((b + 1 - H_GROUP[c]) * NB, (b + 1) * NB)
+                    nc.vector.quantize_mx(
+                        out=codes[:, cols].bitcast(FP8X4),
+                        scales=scales[:, cols],
+                        in_=grouped[:, cols, :].rearrange("p n j -> p (n j)"),
+                    )
+            h_codes[c] = codes
+            h_scales[c] = scales
+
+        w2_codes = {}
+        w2_scales = {}
+
+        def second_weights(key, piece):
+            first, width = W2_QUANT[piece]
+            grouped = keep.tile([P, width, J], BF16, name=f"w2_grouped_{key}{piece}", align_bytes=64)
+            codes = keep.tile([P, width], U32, name=f"w2_codes_{key}{piece}", align_bytes=64)
+            scales = keep.tile([P, width], U8, name=f"w2_scales_{key}{piece}", align_bytes=64)
+            plain_casts(key, first, grouped)
+            nc.vector.quantize_mx(
+                out=codes[:].bitcast(FP8X4), scales=scales[:], in_=grouped[:].rearrange("p m j -> p (m j)")
+            )
+            for m in range(0, width, P):
+                w2_codes[(key, (first + m) // P)] = codes[:, m : m + P]
+                w2_scales[(key, (first + m) // P)] = scales[:, m : m + P]
+
+        for stage in STAGES:
+            if stage == "x":
+                tokens()
+            elif stage[0] in "ab":
+                first_weights(stage[0], int(stage[1]))
+            elif stage[0] == "h":
+                first_layer(int(stage[1]))
+            else:
+                second_weights(stage[0], int(stage[1]))
+
+        for group in L2:
+            banks = []
+            for m, th, parts, engine in group:
+                bank = psum.tile([P, S // parts], F32, name="bank", tag="bank")
+                banks.append(bank)
+            for c, key in enumerate("cd"):
+                for bank, (m, th, parts, engine) in zip(banks, group):
+                    cols = slice(th * (S // parts), (th + 1) * (S // parts))
+                    nc.tensor.matmul_mx(
+                        out=bank[:],
+                        lhsT=w2_codes[(key, m)].bitcast(FP8X4),
+                        lhsT_scale=w2_scales[(key, m)],
+                        rhs=h_codes[c][:, cols].bitcast(FP8X4),
+                        rhs_scale=h_scales[c][:, cols],
+                        start=(c == 0),
+                        stop=(c == 1),
+                    )
+            for bank, (m, th, parts, engine) in zip(banks, group):
+                cols = slice(th * (S // parts), (th + 1) * (S // parts))
+                result = keep.tile([P, S // parts], F32, name=f"result{m}_{th}")
+                copy(engine, result[:], bank[:])
+                nc.sync.dma_start(out=out[m * P : (m + 1) * P, cols], in_=result[:])

@@ -11,7 +11,6 @@ U32 = mybir.dt.uint32
 U16 = mybir.dt.uint16
 U8 = mybir.dt.uint8
 FP8X4 = mybir.dt.float8_e4m3fn_x4
-ADD = mybir.AluOpType.add
 MULT = mybir.AluOpType.mult
 RELU = mybir.ActivationFunctionType.Relu
 
@@ -19,16 +18,16 @@ P = 128
 J = 4
 KP = P * J
 NB = 128
-Q = 256
+HALF = S // 2
 
-ORDER = [["x",0,512],["x",512,512],["a",0,512],["b",0,512],["a",512,512],["b",512,256],["b",768,256],["c",0,512],["d",0,256],["d",256,256]]
-SPLIT = {"x0":[["V",160],["S",96]],"x256":[["V",128],["S",128]],"x512":[["S",256]],"x768":[["V",256]],"a0":[["V",160],["S",96]],"a256":[["S",256]],"b0":[["V",192],["S",64]],"b256":[["S",256]],"a512":[["V",256]],"a768":[["V",224],["S",32]],"b512":[["V",64],["S",192]],"b768":[["S",256]],"c0":[["S",256]],"c256":[["V",96],["S",32]],"c384":[["S",128]],"d0":[["S",256]],"d256":[["S",128]],"d384":[["V",128]]}
-STAGES = ["d0","b1","a0","c0","b0","x","a1","h0","h1","c1","d1","d2","c2"]
-H_GROUP = [4,2]
-X_QUANT = [[0,512],[512,256],[768,256]]
-W2_QUANT = [[0,256],[256,128],[384,128]]
-L2 = [[[0,1,2,"S"]],[[1,0,2,"S"]],[[1,1,2,"V"]],[[0,0,2,"S"]],[[2,0,2,"S"]],[[2,1,2,"V"]],[[3,0,2,"V"]],[[3,1,2,"S"]]]
-G_STEP = 256
+PIECES = {"x":[512,256,256],"a0":[256,256],"b0":[256,256],"a1":[256,256],"b1":[256,256],"c":[256,256],"d":[256,256]}
+LOADS = ["x","a0","b0","a1","b1","c","d"]
+V_SHARE = {"x_0":20,"x_1":6,"x_2":0,"a0_0":0,"a0_1":2,"b0_0":0,"b0_1":16,"a1_0":16,"a1_1":0,"b1_0":2,"b1_1":16,"c_0":12,"c_1":0,"d_0":4,"d_1":0}
+ORDER = [["c","x",0,"V"],["c","x",0,"S"],["q","x",0,512],["c","x",1,"V"],["c","x",1,"S"],["q","x",512,768],["G",0],["c","x",2,"V"],["c","x",2,"S"],["q","x",768,1024],["G",1],["c","a0",0,"V"],["c","a0",0,"S"],["c","a0",1,"V"],["c","a0",1,"S"],["q","a0",0,512],["c","b0",0,"V"],["c","b0",0,"S"],["c","b0",1,"V"],["c","b0",1,"S"],["q","b0",0,512],["g",0,0],["g",0,1],["g",0,2],["c","b1",0,"V"],["c","b1",0,"S"],["g",0,3],["u",0,0],["u",0,1],["c","a1",0,"V"],["c","a1",0,"S"],["u",0,2],["c","a1",1,"V"],["c","a1",1,"S"],["q","a1",0,512],["c","b1",1,"V"],["c","b1",1,"S"],["q","b1",0,512],["g",1,0],["g",1,1],["g",1,2],["c","d",0,"V"],["c","d",0,"S"],["g",1,3],["h",0,0,256],["u",1,0],["u",1,1],["c","c",0,"V"],["c","c",0,"S"],["c","c",1,"V"],["c","c",1,"S"],["h",1,0,256],["q","c",0,256],["q","c",256,512],["q","d",0,256],["o",0,0,256,1],["o",1,0,256,1],["c","d",1,"V"],["c","d",1,"S"],["q","d",256,512],["o",2,0,256,1],["o",3,0,256,1],["u",0,3],["h",0,256,512],["u",1,2],["u",1,3],["h",1,256,512],["o",0,256,512,1],["o",1,256,512,1],["o",2,256,512,1],["o",3,256,512,1]]
+OUT_ENG = {"0_0":"S","1_0":"S","2_0":"S","3_0":"S","0_256":"V","1_256":"S","2_256":"V","3_256":"V"}
+ALIAS = {"gate0_3":"raw_b1_0","gate1_3":"raw_d_0","h_codes10":"raw_b1_256","h_codes00":"raw_a1_256"}
+OUT_BANK = {"0_0":3,"1_0":1,"2_0":2,"3_0":0,"0_256":4,"1_256":5,"2_256":6,"3_256":4}
+Q = 256
 
 
 def tile_picked_pick_glu_relu_srt_e_kernel(tc, xT, w1, w3, w2, offs, out):
@@ -37,104 +36,95 @@ def tile_picked_pick_glu_relu_srt_e_kernel(tc, xT, w1, w3, w2, offs, out):
     def copy(engine, dst, src):
         if engine == "V":
             nc.vector.tensor_copy(out=dst, in_=src)
-        elif engine == "S":
-            nc.scalar.copy(out=dst, in_=src)
         else:
-            nc.gpsimd.tensor_scalar(out=dst, in0=src, scalar1=1.0, scalar2=0.0, op0=MULT, op1=ADD)
+            nc.scalar.copy(out=dst, in_=src)
 
     with ExitStack() as ctx:
         keep = ctx.enter_context(tc.tile_pool(name="keep", bufs=1))
-        psum = ctx.enter_context(tc.psum_pool(name="psum", bufs=8))
+        psum = ctx.enter_context(tc.psum_pool(name="psum", bufs=1))
+
+        def held(shape, dtype, name):
+            return keep.tile(shape, dtype, name=name, tag=ALIAS.get(name, name), align_bytes=64)
 
         offsets = keep.tile([P, S // 16], U16, name="offsets")
+
+        def view(ap):
+            return ap.rearrange("(p j) w -> p j w", j=J)
+
         sources = {
-            "x": xT.rearrange("(p j) w -> p j w", j=J),
-            "a": w1.rearrange("(p j) w -> p j w", j=J),
-            "b": w3.rearrange("(p j) w -> p j w", j=J),
-            "c": w2[:KP, :].rearrange("(p j) w -> p j w", j=J),
-            "d": w2[KP:, :].rearrange("(p j) w -> p j w", j=J),
+            "x": view(xT),
+            "a0": view(w1)[:, :, :KP],
+            "b0": view(w3)[:, :, :KP],
+            "a1": view(w1)[:, :, KP:],
+            "b1": view(w3)[:, :, KP:],
+            "c": view(w2[:KP, :]),
+            "d": view(w2[KP:, :]),
         }
         raws = {}
-        for i, (key, first, width) in enumerate(ORDER):
-            raw = keep.tile([P, J, width], F32, name=f"raw_{key}_{first}")
-            nc.sync.dma_start(out=raw[:], in_=sources[key][:, :, first : first + width])
-            for sub in range(0, width, 128):
-                raws[(key, first + sub)] = (raw, sub)
-            if i == 0:
-                nc.sync.dma_start(offsets[:], offs)
+        for key in LOADS:
+            first = 0
+            for piece, width in enumerate(PIECES[key]):
+                raw = held([P, J, width], F32, f"raw_{key}_{first}")
+                nc.sync.dma_start(out=raw[:], in_=sources[key][:, :, first : first + width])
+                raws[(key, piece)] = (raw, first, width)
+                if key == LOADS[0] and first == 0:
+                    nc.sync.dma_start(offsets[:], offs)
+                first += width
 
-        x_codes = keep.tile([P, T], U32, name="x_codes", align_bytes=64)
-        x_scales = keep.tile([P, T], U8, name="x_scales", align_bytes=64)
+        x_codes = held([P, T], U32, "x_codes")
+        x_scales = held([P, T], U8, "x_scales")
         nc.gpsimd.memset(x_scales[:], 0)
-        xg_codes = keep.tile([P, S], U32, name="xg_codes", align_bytes=64)
-        xg_scales = keep.tile([P, S], U8, name="xg_scales", align_bytes=64)
+        xg_codes = held([P, S], U32, "xg_codes")
+        xg_scales = held([P, S], U8, "xg_scales")
 
-        def shares(key, first):
-            found = []
-            a = 0
-            for engine, n in SPLIT[f"{key}{first}"]:
-                step = G_STEP if engine == "G" else n
-                for s in range(0, n, step):
-                    found.append((engine, a + s, a + min(s + step, n)))
-                a += n
-            return found
+        staged = {}
+        for key in LOADS:
+            if key[0] in "ab":
+                staged[key] = held([P, J, P, J], BF16, f"w_grouped_{key}")
+            else:
+                staged[key] = held([P, sum(PIECES[key]), J], BF16, f"grouped_{key}")
 
-        def plain_casts(key, first, grouped):
-            for engine, a, b in shares(key, first):
-                raw, sub = raws[(key, first)]
-                copy(
-                    engine,
-                    grouped[:, a:b, :].rearrange("p (c i) j -> p c j i", i=4),
-                    raw[:, :, sub + a : sub + b].rearrange("p j (c i) -> p c j i", i=4),
-                )
+        def cast(key, piece, engine, a, b):
+            raw, first, width = raws[(key, piece)]
+            if key[0] in "ab":
+                dst = staged[key][:, :, (first + a) // 4 : (first + b) // 4, :].rearrange("p t m j -> p m j t")
+                src = raw[:, :, a:b].rearrange("p j (m t) -> p m j t", t=4)
+            else:
+                dst = staged[key][:, first + a : first + b, :].rearrange("p (c i) j -> p c j i", i=4)
+                src = raw[:, :, a:b].rearrange("p j (c i) -> p c j i", i=4)
+            copy(engine, dst, src)
 
-        def tokens():
-            for first, width in X_QUANT:
-                grouped = keep.tile([P, width, J], BF16, name=f"x_grouped{first}", align_bytes=64)
-                for sub in range(0, width, Q):
-                    plain_casts("x", first + sub, grouped[:, sub : sub + Q, :])
-                nc.vector.quantize_mx(
-                    out=x_codes[:, first : first + width].bitcast(FP8X4),
-                    scales=x_scales[:, first : first + width],
-                    in_=grouped[:].rearrange("p w j -> p (w j)"),
-                )
-            nc.vector.tensor_copy(xg_codes[:], x_codes[:].indirect(offsets[:]))
-            nc.vector.tensor_copy(xg_scales[:], x_scales[:].indirect(offsets[:]))
+        def gather(half):
+            window = T - HALF + half * HALF
+            cols = slice(half * HALF, (half + 1) * HALF)
+            entries = offsets[:, half * HALF // 16 : (half + 1) * HALF // 16]
+            nc.vector.tensor_copy(xg_codes[:, cols], x_codes[:, :window].indirect(entries))
+            nc.vector.tensor_copy(xg_scales[:, cols], x_scales[:, :window].indirect(entries))
 
         w_codes = {}
         w_scales = {}
+        w_codes["x"] = x_codes
+        w_scales["x"] = x_scales
 
-        def first_weights(w, c):
-            grouped = keep.tile([P, J, P, J], BF16, name=f"w_grouped_{w}{c}", align_bytes=64)
-            codes = keep.tile([P, KP], U32, name=f"w_codes_{w}{c}", align_bytes=64)
-            scales = keep.tile([P, KP], U8, name=f"w_scales_{w}{c}", align_bytes=64)
-            for sub in (0, Q):
-                raw, at = raws[(w, c * KP + sub)]
-                m0 = sub // 4
-                for engine, a, b in shares(w, c * KP + sub):
-                    copy(
-                        engine,
-                        grouped[:, :, m0 + a // 4 : m0 + b // 4, :].rearrange("p t m j -> p m t j"),
-                        raw[:, :, at + a : at + b].rearrange("p j (m t) -> p m t j", t=4),
-                    )
-            nc.vector.quantize_mx(
-                out=codes[:].bitcast(FP8X4), scales=scales[:], in_=grouped[:].rearrange("p t m j -> p (t m j)")
-            )
-            w_codes[(w, c)] = codes
-            w_scales[(w, c)] = scales
+        def quantize(key, a, b):
+            if key not in w_codes:
+                w_codes[key] = held([P, KP], U32, f"w_codes_{key}")
+                w_scales[key] = held([P, KP], U8, f"w_scales_{key}")
+            if key[0] in "ab":
+                src = staged[key][:].rearrange("p t m j -> p (t m j)")
+            else:
+                src = staged[key][:, a:b, :].rearrange("p m j -> p (m j)")
+            nc.vector.quantize_mx(out=w_codes[key][:, a:b].bitcast(FP8X4), scales=w_scales[key][:, a:b], in_=src)
 
-        h_codes = {}
-        h_scales = {}
-
-        def products(w, c, b):
+        def products(key, b):
             cols = slice(b * NB, (b + 1) * NB)
-            bank = psum.tile([P, J, NB], F32, name="bank", tag="bank")
+            bank = psum.tile([P, J, NB], F32, name="bank", tag=f"bank{b + (4 if key[0] == 'b' else 0)}")
             for t in range(J):
                 rows = slice(t * P, (t + 1) * P)
                 nc.tensor.matmul_mx(
                     out=bank[:, t, :],
-                    lhsT=w_codes[(w, c)][:, rows].bitcast(FP8X4),
-                    lhsT_scale=w_scales[(w, c)][:, rows],
+                    lhsT=w_codes[key][:, rows].bitcast(FP8X4),
+                    lhsT_scale=w_scales[key][:, rows],
                     rhs=xg_codes[:, cols].bitcast(FP8X4),
                     rhs_scale=xg_scales[:, cols],
                     start=True,
@@ -142,75 +132,77 @@ def tile_picked_pick_glu_relu_srt_e_kernel(tc, xT, w1, w3, w2, offs, out):
                 )
             return bank[:].rearrange("p t n -> p n t")
 
-        def first_layer(c):
-            grouped = keep.tile([P, S, J], BF16, name=f"h_grouped{c}", align_bytes=64)
-            codes = keep.tile([P, S], U32, name=f"h_codes{c}", align_bytes=64)
-            scales = keep.tile([P, S], U8, name=f"h_scales{c}", align_bytes=64)
-            gates = []
-            for b in range(S // NB):
-                gate = keep.tile([P, NB, J], F32, name=f"gate{c}_{b}")
-                nc.scalar.activation(gate[:], products("a", c, b), RELU)
-                gates.append(gate)
-            for b in range(S // NB):
-                up = products("b", c, b)
-                nc.vector.tensor_tensor(
-                    out=grouped[:, b * NB : (b + 1) * NB, :], in0=gates[b][:], in1=up, op=MULT
-                )
-                if (b + 1) % H_GROUP[c] == 0:
-                    cols = slice((b + 1 - H_GROUP[c]) * NB, (b + 1) * NB)
-                    nc.vector.quantize_mx(
-                        out=codes[:, cols].bitcast(FP8X4),
-                        scales=scales[:, cols],
-                        in_=grouped[:, cols, :].rearrange("p n j -> p (n j)"),
-                    )
-            h_codes[c] = codes
-            h_scales[c] = scales
+        gates = {}
+        h_grouped = {}
+        h_codes = {}
+        h_scales = {}
 
-        w2_codes = {}
-        w2_scales = {}
+        def gate_stage(c, b):
+            gate = held([P, NB, J], F32, f"gate{c}_{b}")
+            nc.scalar.activation(gate[:], products(f"a{c}", b), RELU)
+            gates[(c, b)] = gate
 
-        def second_weights(key, piece):
-            first, width = W2_QUANT[piece]
-            grouped = keep.tile([P, width, J], BF16, name=f"w2_grouped_{key}{piece}", align_bytes=64)
-            codes = keep.tile([P, width], U32, name=f"w2_codes_{key}{piece}", align_bytes=64)
-            scales = keep.tile([P, width], U8, name=f"w2_scales_{key}{piece}", align_bytes=64)
-            plain_casts(key, first, grouped)
-            nc.vector.quantize_mx(
-                out=codes[:].bitcast(FP8X4), scales=scales[:], in_=grouped[:].rearrange("p m j -> p (m j)")
+        def up_stage(c, b):
+            if (c, b // 2) not in h_grouped:
+                h_grouped[(c, b // 2)] = held([P, HALF, J], BF16, f"h_grouped{c}{b // 2}")
+            nc.vector.tensor_tensor(
+                out=h_grouped[(c, b // 2)][:, b % 2 * NB : (b % 2 + 1) * NB, :],
+                in0=gates[(c, b)][:],
+                in1=products(f"b{c}", b),
+                op=MULT,
             )
-            for m in range(0, width, P):
-                w2_codes[(key, (first + m) // P)] = codes[:, m : m + P]
-                w2_scales[(key, (first + m) // P)] = scales[:, m : m + P]
 
-        for stage in STAGES:
-            if stage == "x":
-                tokens()
-            elif stage[0] in "ab":
-                first_weights(stage[0], int(stage[1]))
-            elif stage[0] == "h":
-                first_layer(int(stage[1]))
-            else:
-                second_weights(stage[0], int(stage[1]))
+        def quantize_h(c, a, b):
+            half = a // HALF
+            cols = slice(a % HALF, a % HALF + b - a)
+            if (c, half) not in h_codes:
+                h_codes[(c, half)] = held([P, HALF], U32, f"h_codes{c}{half}")
+                h_scales[(c, half)] = held([P, HALF], U8, f"h_scales{c}{half}")
+            nc.vector.quantize_mx(
+                out=h_codes[(c, half)][:, cols].bitcast(FP8X4),
+                scales=h_scales[(c, half)][:, cols],
+                in_=h_grouped[(c, half)][:, cols, :].rearrange("p n j -> p (n j)"),
+            )
 
-        for group in L2:
-            banks = []
-            for m, th, parts, engine in group:
-                bank = psum.tile([P, S // parts], F32, name="bank", tag="bank")
-                banks.append(bank)
-            for c, key in enumerate("cd"):
-                for bank, (m, th, parts, engine) in zip(banks, group):
-                    cols = slice(th * (S // parts), (th + 1) * (S // parts))
+        def output(m0, count, a, b, engine):
+            cols = slice(a, b)
+            bank = psum.tile([P, count, b - a], F32, name="bank", tag=f"bank{OUT_BANK[f'{m0}_{a}']}")
+            for i in range(count):
+                rows = slice((m0 + i) * P, (m0 + i + 1) * P)
+                for c, key in enumerate("cd"):
                     nc.tensor.matmul_mx(
-                        out=bank[:],
-                        lhsT=w2_codes[(key, m)].bitcast(FP8X4),
-                        lhsT_scale=w2_scales[(key, m)],
-                        rhs=h_codes[c][:, cols].bitcast(FP8X4),
-                        rhs_scale=h_scales[c][:, cols],
+                        out=bank[:, i, :],
+                        lhsT=w_codes[key][:, rows].bitcast(FP8X4),
+                        lhsT_scale=w_scales[key][:, rows],
+                        rhs=h_codes[(c, a // HALF)][:, a % HALF : a % HALF + b - a].bitcast(FP8X4),
+                        rhs_scale=h_scales[(c, a // HALF)][:, a % HALF : a % HALF + b - a],
                         start=(c == 0),
                         stop=(c == 1),
                     )
-            for bank, (m, th, parts, engine) in zip(banks, group):
-                cols = slice(th * (S // parts), (th + 1) * (S // parts))
-                result = keep.tile([P, S // parts], F32, name=f"result{m}_{th}")
-                copy(engine, result[:], bank[:])
-                nc.sync.dma_start(out=out[m * P : (m + 1) * P, cols], in_=result[:])
+            result = held([P, count, b - a], F32, f"result{m0}_{a}")
+            copy(engine, result[:], bank[:])
+            nc.sync.dma_start(
+                out=out[m0 * P : (m0 + count) * P, cols].rearrange("(i p) n -> p i n", p=P), in_=result[:]
+            )
+
+        for stage in ORDER:
+            kind = stage[0]
+            if kind == "c":
+                key, piece, engine = stage[1:]
+                width = PIECES[key][piece]
+                cut = V_SHARE[f"{key}_{piece}"] * 16
+                a, b = (0, cut) if engine == "V" else (cut, width)
+                if b > a:
+                    cast(key, piece, engine, a, b)
+            elif kind == "q":
+                quantize(stage[1], stage[2], stage[3])
+            elif kind == "G":
+                gather(stage[1])
+            elif kind == "g":
+                gate_stage(stage[1], stage[2])
+            elif kind == "u":
+                up_stage(stage[1], stage[2])
+            elif kind == "h":
+                quantize_h(stage[1], stage[2], stage[3])
+            else:
+                output(stage[1], stage[4], stage[2], stage[3], OUT_ENG[f"{stage[1]}_{stage[2]}"])

@@ -20,13 +20,16 @@ KP = P * J
 NB = 128
 HALF = S // 2
 
-PIECES = {"x":[512,256,256],"a0":[256,256],"b0":[256,256],"a1":[256,256],"b1":[256,256],"c":[256,256],"d":[256,256]}
+PIECES = {"x":[512],"a0":[512],"b0":[512],"a1":[512],"b1":[512],"c":[512],"d":[256,256]}
 LOADS = ["x","a0","b0","a1","b1","c","d"]
-V_SHARE = {"x_0":20,"x_1":6,"x_2":0,"a0_0":0,"a0_1":2,"b0_0":0,"b0_1":16,"a1_0":16,"a1_1":0,"b1_0":2,"b1_1":16,"c_0":12,"c_1":0,"d_0":4,"d_1":0}
-ORDER = [["c","x",0,"V"],["c","x",0,"S"],["q","x",0,512],["c","x",1,"V"],["c","x",1,"S"],["q","x",512,768],["G",0],["c","x",2,"V"],["c","x",2,"S"],["q","x",768,1024],["G",1],["c","a0",0,"V"],["c","a0",0,"S"],["c","a0",1,"V"],["c","a0",1,"S"],["q","a0",0,512],["c","b0",0,"V"],["c","b0",0,"S"],["c","b0",1,"V"],["c","b0",1,"S"],["q","b0",0,512],["g",0,0],["g",0,1],["g",0,2],["c","b1",0,"V"],["c","b1",0,"S"],["g",0,3],["u",0,0],["u",0,1],["c","a1",0,"V"],["c","a1",0,"S"],["u",0,2],["c","a1",1,"V"],["c","a1",1,"S"],["q","a1",0,512],["c","b1",1,"V"],["c","b1",1,"S"],["q","b1",0,512],["g",1,0],["g",1,1],["g",1,2],["c","d",0,"V"],["c","d",0,"S"],["g",1,3],["h",0,0,256],["u",1,0],["u",1,1],["c","c",0,"V"],["c","c",0,"S"],["c","c",1,"V"],["c","c",1,"S"],["h",1,0,256],["q","c",0,256],["q","c",256,512],["q","d",0,256],["o",0,0,256,1],["o",1,0,256,1],["c","d",1,"V"],["c","d",1,"S"],["q","d",256,512],["o",2,0,256,1],["o",3,0,256,1],["u",0,3],["h",0,256,512],["u",1,2],["u",1,3],["h",1,256,512],["o",0,256,512,1],["o",1,256,512,1],["o",2,256,512,1],["o",3,256,512,1]]
-OUT_ENG = {"0_0":"S","1_0":"S","2_0":"S","3_0":"S","0_256":"V","1_256":"S","2_256":"V","3_256":"V"}
-ALIAS = {"gate0_3":"raw_b1_0","gate1_3":"raw_d_0","h_codes10":"raw_b1_256","h_codes00":"raw_a1_256"}
-OUT_BANK = {"0_0":3,"1_0":1,"2_0":2,"3_0":0,"0_256":4,"1_256":5,"2_256":6,"3_256":4}
+V_SHARE = {"x_0":44,"x_1":44,"a0_0":8,"b0_0":12,"a1_0":18,"b1_0":16,"c_0":20,"d_0":0,"d_1":4}
+ORDER = [["c","x",0,"V"],["c","x",0,"S"],["G",0],["c","x",1,"V"],["c","x",1,"S"],["G",1],["w"],["c","a0",0,"V"],["c","a0",0,"S"],["q","x",0,512],["q","a0",0,512],["c","b0",0,"V"],["c","b0",0,"S"],["q","b0",0,512],["g",0,0],["g",0,1],["g",0,2],["c","a1",0,"V"],["c","a1",0,"S"],["u",0,0],["u",0,1],["u",0,2],["q","a1",0,512],["g",0,3],["c","b1",0,"V"],["c","b1",0,"S"],["u",0,3],["q","b1",0,512],["g",1,0],["g",1,1],["h",0,0,512],["c","c",0,"V"],["c","c",0,"S"],["u",1,0],["u",1,1],["g",1,2],["q","c",0,512],["h",1,0,256],["c","d",0,"V"],["c","d",0,"S"],["q","d",0,256],["c","d",1,"V"],["c","d",1,"S"],["u",1,2],["q","d",256,512],["g",1,3],["o",0,0,256,1],["o",1,0,256,1],["o",2,0,256,1],["o",3,0,256,1],["h",1,256,384],["u",1,3],["o",0,256,384,2],["o",2,256,384,2],["h",1,384,512],["o",0,384,512,2],["o",2,384,512,2]]
+OUT_ENG = {"0_0":"S","1_0":"S","2_0":"S","3_0":"S","0_256":"S","2_256":"S","0_384":"V","2_384":"S"}
+ALIAS = {"gate1_3":"raw_d_256","gate1_0":"raw_b1_0"}
+OUT_BANK = {"0_0":0,"1_0":1,"2_0":2,"3_0":4,"0_256":5,"2_256":6,"0_384":3,"2_384":7}
+UNITS = {"x":[1024,1024],"a0":[512],"b0":[512],"a1":[512],"b1":[512],"c":[512],"d":[256,256]}
+ROAD = "A"
+WEAVE = "N"
 Q = 256
 
 
@@ -63,48 +66,101 @@ def tile_picked_pick_glu_relu_srt_e_kernel(tc, xT, w1, w3, w2, offs, out):
         raws = {}
         for key in LOADS:
             first = 0
+            if key == "cd":
+                raws["c"] = []
+                raws["d"] = []
+                both = w2.rearrange("(c p j) w -> p c j w", c=2, j=J)
+                for first in (0, 256):
+                    for c, name in enumerate("cd"):
+                        raw = held([P, J, 256], F32, f"raw_{name}_{first}")
+                        nc.sync.dma_start(out=raw[:], in_=both[:, c, :, first : first + 256])
+                        raws[name].append((raw, first, 256))
+                continue
+            raws[key] = []
+            if key == "x" and ROAD == "A":
+                for u in range(2):
+                    raw = held([P, 2, T], F32, f"raw_x_{u}")
+                    nc.sync.dma_start(out=raw[:], in_=sources[key][:, 2 * u : 2 * u + 2, :])
+                    raws[key].append(raw)
+                    if u == 0:
+                        nc.sync.dma_start(offsets[:], offs)
+                continue
             for piece, width in enumerate(PIECES[key]):
                 raw = held([P, J, width], F32, f"raw_{key}_{first}")
                 nc.sync.dma_start(out=raw[:], in_=sources[key][:, :, first : first + width])
-                raws[(key, piece)] = (raw, first, width)
+                raws[key].append((raw, first, width))
                 if key == LOADS[0] and first == 0:
                     nc.sync.dma_start(offsets[:], offs)
                 first += width
 
-        x_codes = held([P, T], U32, "x_codes")
-        x_scales = held([P, T], U8, "x_scales")
-        nc.gpsimd.memset(x_scales[:], 0)
         xg_codes = held([P, S], U32, "xg_codes")
         xg_scales = held([P, S], U8, "xg_scales")
-
+        w_codes = {}
+        w_scales = {}
         staged = {}
-        for key in LOADS:
+        if ROAD == "A":
+            pairs = [held([P, T, 2], BF16, f"pairs{u}") for u in range(2)]
+            picked = held([P, 2, S], U32, "picked")
+            staged["x"] = held([P, S, J], BF16, "grouped_x")
+            w_codes["x"] = xg_codes
+            w_scales["x"] = xg_scales
+        else:
+            x_codes = held([P, T], U32, "x_codes")
+            x_scales = held([P, T], U8, "x_scales")
+            nc.gpsimd.memset(x_scales[:], 0)
+            staged["x"] = held([P, T, J], BF16, "grouped_x")
+            w_codes["x"] = x_codes
+            w_scales["x"] = x_scales
+
+        for key in ("a0", "b0", "a1", "b1", "c", "d"):
             if key[0] in "ab":
                 staged[key] = held([P, J, P, J], BF16, f"w_grouped_{key}")
             else:
                 staged[key] = held([P, sum(PIECES[key]), J], BF16, f"grouped_{key}")
 
-        def cast(key, piece, engine, a, b):
-            raw, first, width = raws[(key, piece)]
+        def cast(key, unit, engine, a, b):
+            if key == "x" and ROAD == "A":
+                dst = pairs[unit][:, a:b, :].rearrange("p (c i) e -> p c e i", i=4)
+                src = raws[key][unit][:, :, a:b].rearrange("p e (c i) -> p c e i", i=4)
+                copy(engine, dst, src)
+                return
+            start = sum(UNITS[key][:unit])
+            a, b = a + start, b + start
+            raw, first, width = [r for r in raws[key] if r[1] <= a < r[1] + r[2]][0]
             if key[0] in "ab":
-                dst = staged[key][:, :, (first + a) // 4 : (first + b) // 4, :].rearrange("p t m j -> p m j t")
-                src = raw[:, :, a:b].rearrange("p j (m t) -> p m j t", t=4)
+                dst = staged[key][:, :, a // 4 : b // 4, :].rearrange("p t m j -> p m j t")
+                src = raw[:, :, a - first : b - first].rearrange("p j (m t) -> p m j t", t=4)
             else:
-                dst = staged[key][:, first + a : first + b, :].rearrange("p (c i) j -> p c j i", i=4)
-                src = raw[:, :, a:b].rearrange("p j (c i) -> p c j i", i=4)
+                dst = staged[key][:, a:b, :].rearrange("p (c i) j -> p c j i", i=4)
+                src = raw[:, :, a - first : b - first].rearrange("p j (c i) -> p c j i", i=4)
             copy(engine, dst, src)
 
         def gather(half):
+            if ROAD == "A":
+                window = pairs[half][:].rearrange("p w e -> p (w e)").bitcast(U32)
+                if WEAVE == "N":
+                    words = staged["x"][:].bitcast(U32)
+                    nc.vector.tensor_copy(words[:, :, half], window.indirect(offsets[:]))
+                else:
+                    nc.vector.tensor_copy(picked[:, half, :], window.indirect(offsets[:]))
+                return
             window = T - HALF + half * HALF
             cols = slice(half * HALF, (half + 1) * HALF)
             entries = offsets[:, half * HALF // 16 : (half + 1) * HALF // 16]
             nc.vector.tensor_copy(xg_codes[:, cols], x_codes[:, :window].indirect(entries))
             nc.vector.tensor_copy(xg_scales[:, cols], x_scales[:, :window].indirect(entries))
 
-        w_codes = {}
-        w_scales = {}
-        w_codes["x"] = x_codes
-        w_scales["x"] = x_scales
+        def weave():
+            if WEAVE == "V":
+                nc.vector.tensor_copy(
+                    out=staged["x"][:].bitcast(F32).rearrange("p (c i) u -> p c u i", i=2),
+                    in_=picked[:].bitcast(F32).rearrange("p u (c i) -> p c u i", i=2),
+                )
+            elif WEAVE == "S":
+                nc.scalar.copy(
+                    out=staged["x"][:].bitcast(U32).rearrange("p (c i) u -> p c u i", i=2),
+                    in_=picked[:].rearrange("p u (c i) -> p c u i", i=2),
+                )
 
         def quantize(key, a, b):
             if key not in w_codes:
@@ -143,25 +199,24 @@ def tile_picked_pick_glu_relu_srt_e_kernel(tc, xT, w1, w3, w2, offs, out):
             gates[(c, b)] = gate
 
         def up_stage(c, b):
-            if (c, b // 2) not in h_grouped:
-                h_grouped[(c, b // 2)] = held([P, HALF, J], BF16, f"h_grouped{c}{b // 2}")
+            if c not in h_grouped:
+                h_grouped[c] = held([P, S, J], BF16, f"h_grouped{c}")
             nc.vector.tensor_tensor(
-                out=h_grouped[(c, b // 2)][:, b % 2 * NB : (b % 2 + 1) * NB, :],
+                out=h_grouped[c][:, b * NB : (b + 1) * NB, :],
                 in0=gates[(c, b)][:],
                 in1=products(f"b{c}", b),
                 op=MULT,
             )
 
         def quantize_h(c, a, b):
-            half = a // HALF
-            cols = slice(a % HALF, a % HALF + b - a)
-            if (c, half) not in h_codes:
-                h_codes[(c, half)] = held([P, HALF], U32, f"h_codes{c}{half}")
-                h_scales[(c, half)] = held([P, HALF], U8, f"h_scales{c}{half}")
+            cols = slice(a, b)
+            if c not in h_codes:
+                h_codes[c] = held([P, S], U32, f"h_codes{c}")
+                h_scales[c] = held([P, S], U8, f"h_scales{c}")
             nc.vector.quantize_mx(
-                out=h_codes[(c, half)][:, cols].bitcast(FP8X4),
-                scales=h_scales[(c, half)][:, cols],
-                in_=h_grouped[(c, half)][:, cols, :].rearrange("p n j -> p (n j)"),
+                out=h_codes[c][:, cols].bitcast(FP8X4),
+                scales=h_scales[c][:, cols],
+                in_=h_grouped[c][:, cols, :].rearrange("p n j -> p (n j)"),
             )
 
         def output(m0, count, a, b, engine):
@@ -174,8 +229,8 @@ def tile_picked_pick_glu_relu_srt_e_kernel(tc, xT, w1, w3, w2, offs, out):
                         out=bank[:, i, :],
                         lhsT=w_codes[key][:, rows].bitcast(FP8X4),
                         lhsT_scale=w_scales[key][:, rows],
-                        rhs=h_codes[(c, a // HALF)][:, a % HALF : a % HALF + b - a].bitcast(FP8X4),
-                        rhs_scale=h_scales[(c, a // HALF)][:, a % HALF : a % HALF + b - a],
+                        rhs=h_codes[c][:, cols].bitcast(FP8X4),
+                        rhs_scale=h_scales[c][:, cols],
                         start=(c == 0),
                         stop=(c == 1),
                     )
@@ -189,13 +244,15 @@ def tile_picked_pick_glu_relu_srt_e_kernel(tc, xT, w1, w3, w2, offs, out):
             kind = stage[0]
             if kind == "c":
                 key, piece, engine = stage[1:]
-                width = PIECES[key][piece]
+                width = UNITS[key][piece]
                 cut = V_SHARE[f"{key}_{piece}"] * 16
                 a, b = (0, cut) if engine == "V" else (cut, width)
                 if b > a:
                     cast(key, piece, engine, a, b)
             elif kind == "q":
                 quantize(stage[1], stage[2], stage[3])
+            elif kind == "w":
+                weave()
             elif kind == "G":
                 gather(stage[1])
             elif kind == "g":

@@ -16,250 +16,184 @@ RELU = mybir.ActivationFunctionType.Relu
 
 P = 128
 J = 4
-KP = P * J
-NB = 128
-HALF = S // 2
+PASS = P * J
+BLOCK = 128
+BLOCKS = S // BLOCK
+TOKENS_OUT = S // 2
+W2_PART = N // 2
+LINE = 4
 
-PIECES = {"x":[512],"a0":[512],"b0":[512],"a1":[512],"b1":[512],"c":[512],"d":[256,256]}
-LOADS = ["x","a0","b0","a1","b1","c","d"]
-V_SHARE = {"x_0":44,"x_1":44,"a0_0":8,"b0_0":12,"a1_0":18,"b1_0":16,"c_0":20,"d_0":0,"d_1":4}
-ORDER = [["c","x",0,"V"],["c","x",0,"S"],["G",0],["c","x",1,"V"],["c","x",1,"S"],["G",1],["w"],["c","a0",0,"V"],["c","a0",0,"S"],["q","x",0,512],["q","a0",0,512],["c","b0",0,"V"],["c","b0",0,"S"],["q","b0",0,512],["g",0,0],["g",0,1],["g",0,2],["c","a1",0,"V"],["c","a1",0,"S"],["u",0,0],["u",0,1],["u",0,2],["q","a1",0,512],["g",0,3],["c","b1",0,"V"],["c","b1",0,"S"],["u",0,3],["q","b1",0,512],["g",1,0],["g",1,1],["h",0,0,512],["c","c",0,"V"],["c","c",0,"S"],["u",1,0],["u",1,1],["g",1,2],["q","c",0,512],["h",1,0,256],["c","d",0,"V"],["c","d",0,"S"],["q","d",0,256],["c","d",1,"V"],["c","d",1,"S"],["u",1,2],["q","d",256,512],["g",1,3],["o",0,0,256,1],["o",1,0,256,1],["o",2,0,256,1],["o",3,0,256,1],["h",1,256,384],["u",1,3],["o",0,256,384,2],["o",2,256,384,2],["h",1,384,512],["o",0,384,512,2],["o",2,384,512,2]]
-OUT_ENG = {"0_0":"S","1_0":"S","2_0":"S","3_0":"S","0_256":"S","2_256":"S","0_384":"V","2_384":"S"}
-ALIAS = {"gate1_3":"raw_d_256","gate1_0":"raw_b1_0"}
-OUT_BANK = {"0_0":0,"1_0":1,"2_0":2,"3_0":4,"0_256":5,"2_256":6,"0_384":3,"2_384":7}
-UNITS = {"x":[1024,1024],"a0":[512],"b0":[512],"a1":[512],"b1":[512],"c":[512],"d":[256,256]}
-ROAD = "A"
-WEAVE = "N"
-Q = 256
+X_VECTOR = 352
+W1_VECTOR = (160, PASS)
+W3_VECTOR = (320, 96)
+W2_VECTOR = ((W2_PART, 128), (0, 0))
 
 
 def tile_picked_pick_glu_relu_srt_e_kernel(tc, xT, w1, w3, w2, offs, out):
     nc = tc.nc
 
-    def copy(engine, dst, src):
-        if engine == "V":
-            nc.vector.tensor_copy(out=dst, in_=src)
-        else:
-            nc.scalar.copy(out=dst, in_=src)
+    def shared_cast(dst, src, vector_share):
+        cut = vector_share // LINE
+        if cut > 0:
+            nc.vector.tensor_copy(out=dst[:, :cut], in_=src[:, :cut])
+        if cut < dst.shape[1]:
+            nc.scalar.copy(out=dst[:, cut:], in_=src[:, cut:])
 
     with ExitStack() as ctx:
         keep = ctx.enter_context(tc.tile_pool(name="keep", bufs=1))
         psum = ctx.enter_context(tc.psum_pool(name="psum", bufs=1))
 
-        def held(shape, dtype, name):
-            return keep.tile(shape, dtype, name=name, tag=ALIAS.get(name, name), align_bytes=64)
+        def held(shape, dtype, name, over=None):
+            return keep.tile(shape, dtype, name=name, tag=over or name, align_bytes=64)
+
+        def load(name, source):
+            raw = held(list(source.shape), F32, name)
+            nc.sync.dma_start(out=raw[:], in_=source)
+            return raw
+
+        def by_word(matrix):
+            return matrix.rearrange("(p j) w -> p j w", j=J)
+
+        def quantised(name, width, over=None):
+            return held([P, width], U32, name + "_codes", over), held([P, width], U8, name + "_scales")
+
+        def quantise(operand, first, staged):
+            codes, scales = operand
+            cols = slice(first, first + staged.shape[1])
+            nc.vector.quantize_mx(
+                out=codes[:, cols].bitcast(FP8X4), scales=scales[:, cols], in_=staged.rearrange("p w j -> p (w j)")
+            )
+
+        def multiply(dst, stationary, rows, moving, cols, start, stop):
+            nc.tensor.matmul_mx(
+                out=dst,
+                lhsT=stationary[0][:, rows].bitcast(FP8X4),
+                lhsT_scale=stationary[1][:, rows],
+                rhs=moving[0][:, cols].bitcast(FP8X4),
+                rhs_scale=moving[1][:, cols],
+                start=start,
+                stop=stop,
+            )
+
+        def cast_plain(name, raw, vector_share):
+            staged = held([P, raw.shape[2], J], BF16, name + "_staged")
+            shared_cast(
+                staged[:].rearrange("p (g i) j -> p g j i", i=LINE),
+                raw.rearrange("p j (g i) -> p g j i", i=LINE),
+                vector_share,
+            )
+            return staged
+
+        def cast_dealt(name, raw, vector_share):
+            staged = held([P, PASS, J], BF16, name + "_staged")
+            shared_cast(
+                staged[:].rearrange("p (t m) j -> p m j t", t=J),
+                raw[:].rearrange("p j (m t) -> p m j t", t=J),
+                vector_share,
+            )
+            return staged
+
+        def quantise_whole(name, staged):
+            operand = quantised(name, PASS)
+            quantise(operand, 0, staged[:])
+            return operand
 
         offsets = keep.tile([P, S // 16], U16, name="offsets")
+        x_raw = [load("x_raw0", by_word(xT)[:, :, : T // 2])]
+        nc.sync.dma_start(offsets[:], offs)
+        x_raw.append(load("x_raw1", by_word(xT)[:, :, T // 2 :]))
+        w1_raw, w3_raw = [], []
+        for c in range(2):
+            w1_raw.append(load(f"w1_raw{c}", by_word(w1)[:, :, c * PASS : (c + 1) * PASS]))
+            w3_raw.append(load(f"w3_raw{c}", by_word(w3)[:, :, c * PASS : (c + 1) * PASS]))
+        parts = [slice(part * W2_PART, (part + 1) * W2_PART) for part in range(2)]
+        w2_first_raw = load("w2_first_raw", by_word(w2[:PASS, :]))
+        w2_raw = [
+            [w2_first_raw[:, :, cols] for cols in parts],
+            [load(f"w2_last_raw{part}", by_word(w2[PASS:, :])[:, :, parts[part]])[:] for part in range(2)],
+        ]
 
-        def view(ap):
-            return ap.rearrange("(p j) w -> p j w", j=J)
+        all_q = quantised("all", T)
+        nc.gpsimd.memset(all_q[1][:], 0)
+        for piece in range(2):
+            quantise(all_q, piece * T // 2, cast_plain(f"x{piece}", x_raw[piece][:], X_VECTOR)[:])
+        x_q = quantised("x", S)
+        for picked, whole in zip(x_q, all_q):
+            nc.vector.tensor_copy(picked[:], whole[:].indirect(offsets[:]))
 
-        sources = {
-            "x": view(xT),
-            "a0": view(w1)[:, :, :KP],
-            "b0": view(w3)[:, :, :KP],
-            "a1": view(w1)[:, :, KP:],
-            "b1": view(w3)[:, :, KP:],
-            "c": view(w2[:KP, :]),
-            "d": view(w2[KP:, :]),
-        }
-        raws = {}
-        for key in LOADS:
-            first = 0
-            if key == "cd":
-                raws["c"] = []
-                raws["d"] = []
-                both = w2.rearrange("(c p j) w -> p c j w", c=2, j=J)
-                for first in (0, 256):
-                    for c, name in enumerate("cd"):
-                        raw = held([P, J, 256], F32, f"raw_{name}_{first}")
-                        nc.sync.dma_start(out=raw[:], in_=both[:, c, :, first : first + 256])
-                        raws[name].append((raw, first, 256))
-                continue
-            raws[key] = []
-            if key == "x" and ROAD == "A":
-                for u in range(2):
-                    raw = held([P, 2, T], F32, f"raw_x_{u}")
-                    nc.sync.dma_start(out=raw[:], in_=sources[key][:, 2 * u : 2 * u + 2, :])
-                    raws[key].append(raw)
-                    if u == 0:
-                        nc.sync.dma_start(offsets[:], offs)
-                continue
-            for piece, width in enumerate(PIECES[key]):
-                raw = held([P, J, width], F32, f"raw_{key}_{first}")
-                nc.sync.dma_start(out=raw[:], in_=sources[key][:, :, first : first + width])
-                raws[key].append((raw, first, width))
-                if key == LOADS[0] and first == 0:
-                    nc.sync.dma_start(offsets[:], offs)
-                first += width
-
-        xg_codes = held([P, S], U32, "xg_codes")
-        xg_scales = held([P, S], U8, "xg_scales")
-        w_codes = {}
-        w_scales = {}
-        staged = {}
-        if ROAD == "A":
-            pairs = [held([P, T, 2], BF16, f"pairs{u}") for u in range(2)]
-            picked = held([P, 2, S], U32, "picked")
-            staged["x"] = held([P, S, J], BF16, "grouped_x")
-            w_codes["x"] = xg_codes
-            w_scales["x"] = xg_scales
-        else:
-            x_codes = held([P, T], U32, "x_codes")
-            x_scales = held([P, T], U8, "x_scales")
-            nc.gpsimd.memset(x_scales[:], 0)
-            staged["x"] = held([P, T, J], BF16, "grouped_x")
-            w_codes["x"] = x_codes
-            w_scales["x"] = x_scales
-
-        for key in ("a0", "b0", "a1", "b1", "c", "d"):
-            if key[0] in "ab":
-                staged[key] = held([P, J, P, J], BF16, f"w_grouped_{key}")
-            else:
-                staged[key] = held([P, sum(PIECES[key]), J], BF16, f"grouped_{key}")
-
-        def cast(key, unit, engine, a, b):
-            if key == "x" and ROAD == "A":
-                dst = pairs[unit][:, a:b, :].rearrange("p (c i) e -> p c e i", i=4)
-                src = raws[key][unit][:, :, a:b].rearrange("p e (c i) -> p c e i", i=4)
-                copy(engine, dst, src)
-                return
-            start = sum(UNITS[key][:unit])
-            a, b = a + start, b + start
-            raw, first, width = [r for r in raws[key] if r[1] <= a < r[1] + r[2]][0]
-            if key[0] in "ab":
-                dst = staged[key][:, :, a // 4 : b // 4, :].rearrange("p t m j -> p m j t")
-                src = raw[:, :, a - first : b - first].rearrange("p j (m t) -> p m j t", t=4)
-            else:
-                dst = staged[key][:, a:b, :].rearrange("p (c i) j -> p c j i", i=4)
-                src = raw[:, :, a - first : b - first].rearrange("p j (c i) -> p c j i", i=4)
-            copy(engine, dst, src)
-
-        def gather(half):
-            if ROAD == "A":
-                window = pairs[half][:].rearrange("p w e -> p (w e)").bitcast(U32)
-                if WEAVE == "N":
-                    words = staged["x"][:].bitcast(U32)
-                    nc.vector.tensor_copy(words[:, :, half], window.indirect(offsets[:]))
-                else:
-                    nc.vector.tensor_copy(picked[:, half, :], window.indirect(offsets[:]))
-                return
-            window = T - HALF + half * HALF
-            cols = slice(half * HALF, (half + 1) * HALF)
-            entries = offsets[:, half * HALF // 16 : (half + 1) * HALF // 16]
-            nc.vector.tensor_copy(xg_codes[:, cols], x_codes[:, :window].indirect(entries))
-            nc.vector.tensor_copy(xg_scales[:, cols], x_scales[:, :window].indirect(entries))
-
-        def weave():
-            if WEAVE == "V":
-                nc.vector.tensor_copy(
-                    out=staged["x"][:].bitcast(F32).rearrange("p (c i) u -> p c u i", i=2),
-                    in_=picked[:].bitcast(F32).rearrange("p u (c i) -> p c u i", i=2),
-                )
-            elif WEAVE == "S":
-                nc.scalar.copy(
-                    out=staged["x"][:].bitcast(U32).rearrange("p (c i) u -> p c u i", i=2),
-                    in_=picked[:].rearrange("p u (c i) -> p c u i", i=2),
-                )
-
-        def quantize(key, a, b):
-            if key not in w_codes:
-                w_codes[key] = held([P, KP], U32, f"w_codes_{key}")
-                w_scales[key] = held([P, KP], U8, f"w_scales_{key}")
-            if key[0] in "ab":
-                src = staged[key][:].rearrange("p t m j -> p (t m j)")
-            else:
-                src = staged[key][:, a:b, :].rearrange("p m j -> p (m j)")
-            nc.vector.quantize_mx(out=w_codes[key][:, a:b].bitcast(FP8X4), scales=w_scales[key][:, a:b], in_=src)
-
-        def products(key, b):
-            cols = slice(b * NB, (b + 1) * NB)
-            bank = psum.tile([P, J, NB], F32, name="bank", tag=f"bank{b + (4 if key[0] == 'b' else 0)}")
+        def first_product(weights, b, bank_number):
+            bank = psum.tile([P, J, BLOCK], F32, name="bank", tag=f"bank{bank_number}")
             for t in range(J):
-                rows = slice(t * P, (t + 1) * P)
-                nc.tensor.matmul_mx(
-                    out=bank[:, t, :],
-                    lhsT=w_codes[key][:, rows].bitcast(FP8X4),
-                    lhsT_scale=w_scales[key][:, rows],
-                    rhs=xg_codes[:, cols].bitcast(FP8X4),
-                    rhs_scale=xg_scales[:, cols],
-                    start=True,
-                    stop=True,
+                multiply(
+                    bank[:, t, :], weights, slice(t * P, (t + 1) * P), x_q, slice(b * BLOCK, (b + 1) * BLOCK), True, True
                 )
             return bank[:].rearrange("p t n -> p n t")
 
-        gates = {}
-        h_grouped = {}
-        h_codes = {}
-        h_scales = {}
+        def gate(dst, weights, b):
+            nc.scalar.activation(dst, first_product(weights, b, b), RELU)
 
-        def gate_stage(c, b):
-            gate = held([P, NB, J], F32, f"gate{c}_{b}")
-            nc.scalar.activation(gate[:], products(f"a{c}", b), RELU)
-            gates[(c, b)] = gate
-
-        def up_stage(c, b):
-            if c not in h_grouped:
-                h_grouped[c] = held([P, S, J], BF16, f"h_grouped{c}")
+        def hidden(staged, gate_values, weights, b):
             nc.vector.tensor_tensor(
-                out=h_grouped[c][:, b * NB : (b + 1) * NB, :],
-                in0=gates[(c, b)][:],
-                in1=products(f"b{c}", b),
+                out=staged[:, b * BLOCK : (b + 1) * BLOCK, :],
+                in0=gate_values,
+                in1=first_product(weights, b, BLOCKS + b),
                 op=MULT,
             )
 
-        def quantize_h(c, a, b):
-            cols = slice(a, b)
-            if c not in h_codes:
-                h_codes[c] = held([P, S], U32, f"h_codes{c}")
-                h_scales[c] = held([P, S], U8, f"h_scales{c}")
-            nc.vector.quantize_mx(
-                out=h_codes[c][:, cols].bitcast(FP8X4),
-                scales=h_scales[c][:, cols],
-                in_=h_grouped[c][:, cols, :].rearrange("p n j -> p (n j)"),
-            )
+        def cast_w2(c, part):
+            return cast_plain(f"w2_{c}_{part}", w2_raw[c][part], W2_VECTOR[c][part])
 
-        def output(m0, count, a, b, engine):
-            cols = slice(a, b)
-            bank = psum.tile([P, count, b - a], F32, name="bank", tag=f"bank{OUT_BANK[f'{m0}_{a}']}")
-            for i in range(count):
-                rows = slice((m0 + i) * P, (m0 + i + 1) * P)
-                for c, key in enumerate("cd"):
-                    nc.tensor.matmul_mx(
-                        out=bank[:, i, :],
-                        lhsT=w_codes[key][:, rows].bitcast(FP8X4),
-                        lhsT_scale=w_scales[key][:, rows],
-                        rhs=h_codes[c][:, cols].bitcast(FP8X4),
-                        rhs_scale=h_scales[c][:, cols],
-                        start=(c == 0),
-                        stop=(c == 1),
-                    )
-            result = held([P, count, b - a], F32, f"result{m0}_{a}")
-            copy(engine, result[:], bank[:])
-            nc.sync.dma_start(
-                out=out[m0 * P : (m0 + count) * P, cols].rearrange("(i p) n -> p i n", p=P), in_=result[:]
-            )
+        def quantise_w2(c, part, staged):
+            quantise(w2_q[c], part * W2_PART, staged[:])
 
-        for stage in ORDER:
-            kind = stage[0]
-            if kind == "c":
-                key, piece, engine = stage[1:]
-                width = UNITS[key][piece]
-                cut = V_SHARE[f"{key}_{piece}"] * 16
-                a, b = (0, cut) if engine == "V" else (cut, width)
-                if b > a:
-                    cast(key, piece, engine, a, b)
-            elif kind == "q":
-                quantize(stage[1], stage[2], stage[3])
-            elif kind == "w":
-                weave()
-            elif kind == "G":
-                gather(stage[1])
-            elif kind == "g":
-                gate_stage(stage[1], stage[2])
-            elif kind == "u":
-                up_stage(stage[1], stage[2])
-            elif kind == "h":
-                quantize_h(stage[1], stage[2], stage[3])
-            else:
-                output(stage[1], stage[4], stage[2], stage[3], OUT_ENG[f"{stage[1]}_{stage[2]}"])
+        last = BLOCKS - 1
+
+        w1_q = quantise_whole("w1_0", cast_dealt("w1_0", w1_raw[0], W1_VECTOR[0]))
+        w3_q = quantise_whole("w3_0", cast_dealt("w3_0", w3_raw[0], W3_VECTOR[0]))
+        gates = [held([P, BLOCK, J], F32, f"gate0_{b}")[:] for b in range(BLOCKS)]
+        for b in range(BLOCKS):
+            gate(gates[b], w1_q, b)
+        w1_staged = cast_dealt("w1_1", w1_raw[1], W1_VECTOR[1])
+        h_first = held([P, S, J], BF16, "h_first", over="w1_raw1")
+        hidden(h_first, gates[0], w3_q, 0)
+        w1_q = quantise_whole("w1_1", w1_staged)
+        hidden(h_first, gates[1], w3_q, 1)
+        w3_staged = cast_dealt("w3_1", w3_raw[1], W3_VECTOR[1])
+        for b in range(2, BLOCKS):
+            hidden(h_first, gates[b], w3_q, b)
+        w3_q = quantise_whole("w3_1", w3_staged)
+        h_q = [quantised("h0", S, over="w3_1_staged")]
+        quantise(h_q[0], 0, h_first[:])
+
+        early_gates = held([P, last, BLOCK, J], F32, "gates1", over="w3_raw1")
+        for b in range(last):
+            gate(early_gates[:, b, :, :], w1_q, b)
+        w2_q = [quantised(f"w2_{c}", N) for c in range(2)]
+        w2_staged = [cast_w2(0, part) for part in range(2)]
+        h_second = held([P, S, J], BF16, "h_second")
+        for b in range(2):
+            hidden(h_second, early_gates[:, b, :, :], w3_q, b)
+            quantise_w2(0, b, w2_staged[b])
+        h_q.append(quantised("h1", S))
+        quantise(h_q[1], 0, h_second[:, :TOKENS_OUT, :])
+        quantise_w2(1, 0, cast_w2(1, 0))
+        last_gate = held([P, BLOCK, J], F32, "gate1_last", over="w2_last_raw0")
+        gate(last_gate[:], w1_q, last)
+        w2_last_staged = cast_w2(1, 1)
+        hidden(h_second, early_gates[:, last - 1, :, :], w3_q, last - 1)
+        hidden(h_second, last_gate[:], w3_q, last)
+        quantise_w2(1, 1, w2_last_staged)
+        quantise(h_q[1], TOKENS_OUT, h_second[:, TOKENS_OUT:, :])
+
+        free_banks = [0, 1, 2, 4, 5, 3, 6, 7]
+        for half in range(2):
+            cols = slice(half * TOKENS_OUT, (half + 1) * TOKENS_OUT)
+            for m in range(N // P):
+                rows = slice(m * P, (m + 1) * P)
+                bank = psum.tile([P, TOKENS_OUT], F32, name="bank", tag=f"bank{free_banks[half * (N // P) + m]}")
+                for c in range(2):
+                    multiply(bank[:], w2_q[c], rows, h_q[c], cols, c == 0, c == 1)
+                result = held([P, TOKENS_OUT], F32, f"result{m}_{half}")
+                copy = nc.vector.tensor_copy if half == 1 and m % 2 == 0 else nc.scalar.copy
+                copy(out=result[:], in_=bank[:])
+                nc.sync.dma_start(out=out[rows, cols], in_=result[:])

@@ -181,19 +181,26 @@ def tile_picked_pick_glu_relu_srt_e_kernel(tc, xT, w1, w3, w2, offs, out):
         gate(last_gate[:], w1_q, last)
         w2_last_staged = cast_w2(1, 1)
         hidden(h_second, early_gates[:, last - 1, :, :], w3_q, last - 1)
-        hidden(h_second, last_gate[:], w3_q, last)
         quantise_w2(1, 1, w2_last_staged)
-        quantise(h_q[1], TOKENS_OUT, h_second[:, TOKENS_OUT:, :])
+        quantise(h_q[1], (last - 1) * BLOCK, h_second[:, (last - 1) * BLOCK : last * BLOCK, :])
+        hidden(h_second, last_gate[:], w3_q, last)
+        quantise(h_q[1], last * BLOCK, h_second[:, last * BLOCK :, :])
 
-        free_banks = [0, 1, 2, 4, 5, 3, 6, 7]
-        for half in range(2):
-            cols = slice(half * TOKENS_OUT, (half + 1) * TOKENS_OUT)
-            for m in range(N // P):
-                rows = slice(m * P, (m + 1) * P)
-                bank = psum.tile([P, TOKENS_OUT], F32, name="bank", tag=f"bank{free_banks[half * (N // P) + m]}")
+        def output(first_tile, tiles, cols, bank_number, copy):
+            width = cols.stop - cols.start
+            bank = psum.tile([P, tiles, width], F32, name="bank", tag=f"bank{bank_number}")
+            for i in range(tiles):
+                rows = slice((first_tile + i) * P, (first_tile + i + 1) * P)
                 for c in range(2):
-                    multiply(bank[:], w2_q[c], rows, h_q[c], cols, c == 0, c == 1)
-                result = held([P, TOKENS_OUT], F32, f"result{m}_{half}")
-                copy = nc.vector.tensor_copy if half == 1 and m % 2 == 0 else nc.scalar.copy
-                copy(out=result[:], in_=bank[:])
-                nc.sync.dma_start(out=out[rows, cols], in_=result[:])
+                    multiply(bank[:, i, :], w2_q[c], rows, h_q[c], cols, c == 0, c == 1)
+            result = held([P, tiles, width], F32, f"result{first_tile}_{cols.start}")
+            copy(out=result[:], in_=bank[:])
+            rows = slice(first_tile * P, (first_tile + tiles) * P)
+            nc.sync.dma_start(out=out[rows, cols].rearrange("(i p) n -> p i n", p=P), in_=result[:])
+
+        for m, bank_number in enumerate((0, 1, 2, 4)):
+            output(m, 1, slice(0, TOKENS_OUT), bank_number, nc.scalar.copy)
+        for pair, bank_number in enumerate((5, 6)):
+            output(2 * pair, 2, slice((last - 1) * BLOCK, last * BLOCK), bank_number, nc.scalar.copy)
+        for pair, (bank_number, copy) in enumerate(((3, nc.vector.tensor_copy), (7, nc.scalar.copy))):
+            output(2 * pair, 2, slice(last * BLOCK, S), bank_number, copy)

@@ -24,9 +24,9 @@ W2_PART = N // 2
 LINE = 4
 
 X_VECTOR = 352
-W1_VECTOR = (160, PASS)
-W3_VECTOR = (320, 96)
-W2_VECTOR = ((W2_PART, 128), (0, 0))
+W1_VECTOR = (112, PASS)
+W3_VECTOR = (272, 80)
+W2_VECTOR = ((160, W2_PART), (0, 0))
 
 
 def tile_picked_pick_glu_relu_srt_e_kernel(tc, xT, w1, w3, w2, offs, out):
@@ -150,6 +150,9 @@ def tile_picked_pick_glu_relu_srt_e_kernel(tc, xT, w1, w3, w2, offs, out):
 
         w1_q = quantise_whole("w1_0", cast_dealt("w1_0", w1_raw[0], W1_VECTOR[0]))
         w3_q = quantise_whole("w3_0", cast_dealt("w3_0", w3_raw[0], W3_VECTOR[0]))
+        for warm_up in range(2):
+            unread = psum.tile([P, S], F32, name="bank", tag="bank7")
+            multiply(unread[:], x_q, slice(0, P), x_q, slice(0, S), True, True)
         gates = [held([P, BLOCK, J], F32, f"gate0_{b}")[:] for b in range(BLOCKS)]
         for b in range(BLOCKS):
             gate(gates[b], w1_q, b)
@@ -177,9 +180,9 @@ def tile_picked_pick_glu_relu_srt_e_kernel(tc, xT, w1, w3, w2, offs, out):
         h_q.append(quantised("h1", S))
         quantise(h_q[1], 0, h_second[:, :TOKENS_OUT, :])
         quantise_w2(1, 0, cast_w2(1, 0))
-        last_gate = held([P, BLOCK, J], F32, "gate1_last", over="w2_last_raw0")
-        gate(last_gate[:], w1_q, last)
         w2_last_staged = cast_w2(1, 1)
+        last_gate = held([P, BLOCK, J], F32, "gate1_last", over="w2_last_raw1")
+        gate(last_gate[:], w1_q, last)
         hidden(h_second, early_gates[:, last - 1, :, :], w3_q, last - 1)
         quantise_w2(1, 1, w2_last_staged)
         quantise(h_q[1], (last - 1) * BLOCK, h_second[:, (last - 1) * BLOCK : last * BLOCK, :])
@@ -202,5 +205,14 @@ def tile_picked_pick_glu_relu_srt_e_kernel(tc, xT, w1, w3, w2, offs, out):
             output(m, 1, slice(0, TOKENS_OUT), bank_number, nc.scalar.copy)
         for pair, bank_number in enumerate((5, 6)):
             output(2 * pair, 2, slice((last - 1) * BLOCK, last * BLOCK), bank_number, nc.scalar.copy)
-        for pair, (bank_number, copy) in enumerate(((3, nc.vector.tensor_copy), (7, nc.scalar.copy))):
-            output(2 * pair, 2, slice(last * BLOCK, S), bank_number, copy)
+        cols = slice(last * BLOCK, S)
+        banks = [psum.tile([P, BLOCK], F32, name="bank", tag=f"bank{number}") for number in (3, 0, 1, 7)]
+        for c in range(2):
+            for m in range(J):
+                multiply(banks[m][:], w2_q[c], slice(m * P, (m + 1) * P), h_q[c], cols, c == 0, c == 1)
+        for pair in range(2):
+            result = held([P, 2, BLOCK], F32, f"last_result{pair}")
+            nc.vector.tensor_copy(out=result[:, 0, :], in_=banks[2 * pair][:])
+            nc.scalar.copy(out=result[:, 1, :], in_=banks[2 * pair + 1][:])
+            rows = slice(2 * pair * P, 2 * (pair + 1) * P)
+            nc.sync.dma_start(out=out[rows, cols].rearrange("(i p) n -> p i n", p=P), in_=result[:])

@@ -23,10 +23,11 @@ TOKENS_OUT = S // 2
 W2_PART = N // 2
 LINE = 4
 
-X_VECTOR = 352
-W1_VECTOR = (112, PASS)
-W3_VECTOR = (272, 80)
-W2_VECTOR = ((160, W2_PART), (0, 0))
+X_LOADS = (512, 256, 256)
+X_VECTOR = (352, 176, 192)
+W1_VECTOR = (192, 336)
+W3_VECTOR = (304, 176)
+W2_VECTOR = ((W2_PART, 32), (0, 96))
 
 
 def tile_picked_pick_glu_relu_srt_e_kernel(tc, xT, w1, w3, w2, offs, out):
@@ -99,13 +100,17 @@ def tile_picked_pick_glu_relu_srt_e_kernel(tc, xT, w1, w3, w2, offs, out):
             return operand
 
         offsets = keep.tile([P, S // 16], U16, name="offsets")
-        x_raw = [load("x_raw0", by_word(xT)[:, :, : T // 2])]
+        x_first = [sum(X_LOADS[:piece]) for piece in range(len(X_LOADS) + 1)]
+        x_raw = [load("x_raw0", by_word(xT)[:, :, : x_first[1]])]
         nc.sync.dma_start(offsets[:], offs)
-        x_raw.append(load("x_raw1", by_word(xT)[:, :, T // 2 :]))
-        w1_raw, w3_raw = [], []
-        for c in range(2):
-            w1_raw.append(load(f"w1_raw{c}", by_word(w1)[:, :, c * PASS : (c + 1) * PASS]))
-            w3_raw.append(load(f"w3_raw{c}", by_word(w3)[:, :, c * PASS : (c + 1) * PASS]))
+        for piece in range(1, len(X_LOADS)):
+            x_raw.append(load(f"x_raw{piece}", by_word(xT)[:, :, x_first[piece] : x_first[piece + 1]]))
+        w1_first_raw = load("w1_first_raw", by_word(w1)[:, :, :PASS])
+        w3_raw = [load("w3_raw0", by_word(w3)[:, :, :PASS])]
+        w1_cut = PASS + W1_VECTOR[1]
+        w1_vector_raw = load("w1_vector_raw", by_word(w1)[:, :, PASS:w1_cut])
+        w1_scalar_raw = load("w1_scalar_raw", by_word(w1)[:, :, w1_cut:])
+        w3_raw.append(load("w3_raw1", by_word(w3)[:, :, PASS:]))
         parts = [slice(part * W2_PART, (part + 1) * W2_PART) for part in range(2)]
         w2_first_raw = load("w2_first_raw", by_word(w2[:PASS, :]))
         w2_raw = [
@@ -115,8 +120,8 @@ def tile_picked_pick_glu_relu_srt_e_kernel(tc, xT, w1, w3, w2, offs, out):
 
         all_q = quantised("all", T)
         nc.gpsimd.memset(all_q[1][:], 0)
-        for piece in range(2):
-            quantise(all_q, piece * T // 2, cast_plain(f"x{piece}", x_raw[piece][:], X_VECTOR)[:])
+        for piece in range(len(X_LOADS)):
+            quantise(all_q, x_first[piece], cast_plain(f"x{piece}", x_raw[piece][:], X_VECTOR[piece])[:])
         x_q = quantised("x", S)
         for picked, whole in zip(x_q, all_q):
             nc.vector.tensor_copy(picked[:], whole[:].indirect(offsets[:]))
@@ -148,16 +153,21 @@ def tile_picked_pick_glu_relu_srt_e_kernel(tc, xT, w1, w3, w2, offs, out):
 
         last = BLOCKS - 1
 
-        w1_q = quantise_whole("w1_0", cast_dealt("w1_0", w1_raw[0], W1_VECTOR[0]))
+        w1_q = quantise_whole("w1_0", cast_dealt("w1_0", w1_first_raw, W1_VECTOR[0]))
         w3_q = quantise_whole("w3_0", cast_dealt("w3_0", w3_raw[0], W3_VECTOR[0]))
         for warm_up in range(2):
             unread = psum.tile([P, S], F32, name="bank", tag="bank7")
             multiply(unread[:], x_q, slice(0, P), x_q, slice(0, S), True, True)
-        gates = [held([P, BLOCK, J], F32, f"gate0_{b}")[:] for b in range(BLOCKS)]
+        first_gates = held([P, BLOCKS, BLOCK, J], F32, "gates0", over="w3_raw0")
+        gates = [first_gates[:, b, :, :] for b in range(BLOCKS)]
         for b in range(BLOCKS):
             gate(gates[b], w1_q, b)
-        w1_staged = cast_dealt("w1_1", w1_raw[1], W1_VECTOR[1])
-        h_first = held([P, S, J], BF16, "h_first", over="w1_raw1")
+        w1_staged = held([P, PASS, J], BF16, "w1_1_staged")
+        dealt = w1_staged[:].rearrange("p (t m) j -> p m j t", t=J)
+        cut = W1_VECTOR[1] // J
+        nc.vector.tensor_copy(out=dealt[:, :cut], in_=w1_vector_raw[:].rearrange("p j (m t) -> p m j t", t=J))
+        nc.scalar.copy(out=dealt[:, cut:], in_=w1_scalar_raw[:].rearrange("p j (m t) -> p m j t", t=J))
+        h_first = held([P, S, J], BF16, "h_first", over="w1_vector_raw")
         hidden(h_first, gates[0], w3_q, 0)
         w1_q = quantise_whole("w1_1", w1_staged)
         hidden(h_first, gates[1], w3_q, 1)
@@ -165,10 +175,10 @@ def tile_picked_pick_glu_relu_srt_e_kernel(tc, xT, w1, w3, w2, offs, out):
         for b in range(2, BLOCKS):
             hidden(h_first, gates[b], w3_q, b)
         w3_q = quantise_whole("w3_1", w3_staged)
-        h_q = [quantised("h0", S, over="w3_1_staged")]
+        h_q = [quantised("h0", S)]
         quantise(h_q[0], 0, h_first[:])
 
-        early_gates = held([P, last, BLOCK, J], F32, "gates1", over="w3_raw1")
+        early_gates = held([P, last, BLOCK, J], F32, "gates1")
         for b in range(last):
             gate(early_gates[:, b, :, :], w1_q, b)
         w2_q = [quantised(f"w2_{c}", N) for c in range(2)]
@@ -181,7 +191,7 @@ def tile_picked_pick_glu_relu_srt_e_kernel(tc, xT, w1, w3, w2, offs, out):
         quantise(h_q[1], 0, h_second[:, :TOKENS_OUT, :])
         quantise_w2(1, 0, cast_w2(1, 0))
         w2_last_staged = cast_w2(1, 1)
-        last_gate = held([P, BLOCK, J], F32, "gate1_last", over="w2_last_raw1")
+        last_gate = held([P, BLOCK, J], F32, "gate1_last", over="w2_last_raw0")
         gate(last_gate[:], w1_q, last)
         hidden(h_second, early_gates[:, last - 1, :, :], w3_q, last - 1)
         quantise_w2(1, 1, w2_last_staged)
@@ -203,8 +213,8 @@ def tile_picked_pick_glu_relu_srt_e_kernel(tc, xT, w1, w3, w2, offs, out):
 
         for m, bank_number in enumerate((0, 1, 2, 4)):
             output(m, 1, slice(0, TOKENS_OUT), bank_number, nc.scalar.copy)
-        for pair, bank_number in enumerate((5, 6)):
-            output(2 * pair, 2, slice((last - 1) * BLOCK, last * BLOCK), bank_number, nc.scalar.copy)
+        for pair, (bank_number, copy) in enumerate(((5, nc.scalar.copy), (6, nc.vector.tensor_copy))):
+            output(2 * pair, 2, slice((last - 1) * BLOCK, last * BLOCK), bank_number, copy)
         cols = slice(last * BLOCK, S)
         banks = [psum.tile([P, BLOCK], F32, name="bank", tag=f"bank{number}") for number in (3, 0, 1, 7)]
         for c in range(2):

@@ -79,8 +79,8 @@ def tile_picked_pick_glu_relu_srt_e_kernel(tc, xT, w1, w3, w2, offs, out):
         def cast_plain(name, raw, vector_share):
             staged = held([P, raw.shape[2], J], BF16, name + "_staged")
             shared_cast(
-                staged[:].rearrange("p (g i) j -> p g j i", i=LINE),
-                raw.rearrange("p j (g i) -> p g j i", i=LINE),
+                staged[:].rearrange("p (g i) (u e) -> p g u i e", i=LINE, e=2),
+                raw.rearrange("p (u e) (g i) -> p g u i e", i=LINE, e=2),
                 vector_share,
             )
             return staged
@@ -88,8 +88,8 @@ def tile_picked_pick_glu_relu_srt_e_kernel(tc, xT, w1, w3, w2, offs, out):
         def cast_dealt(name, raw, vector_share):
             staged = held([P, PASS, J], BF16, name + "_staged")
             shared_cast(
-                staged[:].rearrange("p (t m) j -> p m j t", t=J),
-                raw[:].rearrange("p j (m t) -> p m j t", t=J),
+                staged[:].rearrange("p (t m) (u e) -> p m u t e", t=J, e=2),
+                raw[:].rearrange("p (u e) (m t) -> p m u t e", t=J, e=2),
                 vector_share,
             )
             return staged
@@ -163,10 +163,10 @@ def tile_picked_pick_glu_relu_srt_e_kernel(tc, xT, w1, w3, w2, offs, out):
         for b in range(BLOCKS):
             gate(gates[b], w1_q, b)
         w1_staged = held([P, PASS, J], BF16, "w1_1_staged")
-        dealt = w1_staged[:].rearrange("p (t m) j -> p m j t", t=J)
+        dealt = w1_staged[:].rearrange("p (t m) (u e) -> p m u t e", t=J, e=2)
         cut = W1_VECTOR[1] // J
-        nc.vector.tensor_copy(out=dealt[:, :cut], in_=w1_vector_raw[:].rearrange("p j (m t) -> p m j t", t=J))
-        nc.scalar.copy(out=dealt[:, cut:], in_=w1_scalar_raw[:].rearrange("p j (m t) -> p m j t", t=J))
+        nc.vector.tensor_copy(out=dealt[:, :cut], in_=w1_vector_raw[:].rearrange("p (u e) (m t) -> p m u t e", t=J, e=2))
+        nc.scalar.copy(out=dealt[:, cut:], in_=w1_scalar_raw[:].rearrange("p (u e) (m t) -> p m u t e", t=J, e=2))
         h_first = held([P, S, J], BF16, "h_first", over="w1_vector_raw")
         hidden(h_first, gates[0], w3_q, 0)
         w1_q = quantise_whole("w1_1", w1_staged)
@@ -215,14 +215,5 @@ def tile_picked_pick_glu_relu_srt_e_kernel(tc, xT, w1, w3, w2, offs, out):
             output(m, 1, slice(0, TOKENS_OUT), bank_number, nc.scalar.copy)
         for pair, (bank_number, copy) in enumerate(((5, nc.scalar.copy), (6, nc.vector.tensor_copy))):
             output(2 * pair, 2, slice((last - 1) * BLOCK, last * BLOCK), bank_number, copy)
-        cols = slice(last * BLOCK, S)
-        banks = [psum.tile([P, BLOCK], F32, name="bank", tag=f"bank{number}") for number in (3, 0, 1, 7)]
-        for c in range(2):
-            for m in range(J):
-                multiply(banks[m][:], w2_q[c], slice(m * P, (m + 1) * P), h_q[c], cols, c == 0, c == 1)
-        for pair in range(2):
-            result = held([P, 2, BLOCK], F32, f"last_result{pair}")
-            nc.vector.tensor_copy(out=result[:, 0, :], in_=banks[2 * pair][:])
-            nc.scalar.copy(out=result[:, 1, :], in_=banks[2 * pair + 1][:])
-            rows = slice(2 * pair * P, 2 * (pair + 1) * P)
-            nc.sync.dma_start(out=out[rows, cols].rearrange("(i p) n -> p i n", p=P), in_=result[:])
+        for pair, (bank_number, copy) in enumerate(((3, nc.vector.tensor_copy), (7, nc.scalar.copy))):
+            output(2 * pair, 2, slice(last * BLOCK, S), bank_number, copy)

@@ -13,39 +13,34 @@ U8 = mybir.dt.uint8
 FP8X4 = mybir.dt.float8_e4m3fn_x4
 MULT = mybir.AluOpType.mult
 RELU = mybir.ActivationFunctionType.Relu
+COPY = mybir.ActivationFunctionType.Copy
 
 P = 128
 J = 4
 PASS = P * J
 BLOCK = 128
 BLOCKS = S // BLOCK
-TOKENS_OUT = S // 2
+HALF = S // 2
 W2_PART = N // 2
 LINE = 4
+STRIPE = 16
 
-X_LOADS = (512, 256, 256)
-X_VECTOR = (352, 176, 192)
-W1_VECTOR = (192, 336)
-W3_VECTOR = (304, 176)
-W2_VECTOR = ((W2_PART, 32), (0, 96))
+W1_VECTOR = 336
+W3_FIRST_VECTOR = (80, 128)
+W3_VECTOR = 224
+W2_LAST_VECTOR = 96
 
 
 def tile_picked_pick_glu_relu_srt_e_kernel(tc, xT, w1, w3, w2, offs, out):
     nc = tc.nc
 
-    def shared_cast(dst, src, vector_share):
-        cut = vector_share // LINE
-        if cut > 0:
-            nc.vector.tensor_copy(out=dst[:, :cut], in_=src[:, :cut])
-        if cut < dst.shape[1]:
-            nc.scalar.copy(out=dst[:, cut:], in_=src[:, cut:])
-
     with ExitStack() as ctx:
         keep = ctx.enter_context(tc.tile_pool(name="keep", bufs=1))
+        tail = ctx.enter_context(tc.tile_pool(name="tail", bufs=1))
         psum = ctx.enter_context(tc.psum_pool(name="psum", bufs=1))
 
         def held(shape, dtype, name, over=None):
-            return keep.tile(shape, dtype, name=name, tag=over or name, align_bytes=64)
+            return keep.tile(shape, dtype, name=name, tag=over or name, align_bytes=256)
 
         def load(name, source):
             raw = held(list(source.shape), F32, name)
@@ -54,6 +49,13 @@ def tile_picked_pick_glu_relu_srt_e_kernel(tc, xT, w1, w3, w2, offs, out):
 
         def by_word(matrix):
             return matrix.rearrange("(p j) w -> p j w", j=J)
+
+        def shared_cast(dst, src, vector_share):
+            cut = vector_share // LINE
+            if cut > 0:
+                nc.vector.tensor_copy(out=dst[:, :cut], in_=src[:, :cut])
+            if cut < dst.shape[1]:
+                nc.scalar.copy(out=dst[:, cut:], in_=src[:, cut:])
 
         def quantised(name, width, over=None):
             return held([P, width], U32, name + "_codes", over), held([P, width], U8, name + "_scales")
@@ -85,46 +87,56 @@ def tile_picked_pick_glu_relu_srt_e_kernel(tc, xT, w1, w3, w2, offs, out):
             )
             return staged
 
-        def cast_dealt(name, raw, vector_share):
-            staged = held([P, PASS, J], BF16, name + "_staged")
+        def cast_dealt(staged, first, raw, vector_share):
+            groups = slice(first // J, (first + raw.shape[2]) // J)
             shared_cast(
-                staged[:].rearrange("p (t m) (u e) -> p m u t e", t=J, e=2),
+                staged[:].rearrange("p (t m) (u e) -> p m u t e", t=J, e=2)[:, groups],
                 raw[:].rearrange("p (u e) (m t) -> p m u t e", t=J, e=2),
                 vector_share,
             )
+
+        def stage_half(name, raw, vector_share):
+            staged = held([P, PASS, J], BF16, name + "_staged")
+            cast_dealt(staged, 0, raw, vector_share)
             return staged
 
-        def quantise_whole(name, staged):
+        def quantise_in(name, staged, pieces):
             operand = quantised(name, PASS)
-            quantise(operand, 0, staged[:])
+            width = PASS // pieces
+            for piece in range(pieces):
+                quantise(operand, piece * width, staged[:, piece * width : (piece + 1) * width, :])
             return operand
 
-        offsets = keep.tile([P, S // 16], U16, name="offsets")
-        x_first = [sum(X_LOADS[:piece]) for piece in range(len(X_LOADS) + 1)]
-        x_raw = [load("x_raw0", by_word(xT)[:, :, : x_first[1]])]
+        w1_raw = load("w1_raw0", by_word(w1)[:, :, :PASS])
+        offsets = keep.tile([P, S // STRIPE], U16, name="offsets")
         nc.sync.dma_start(offsets[:], offs)
-        for piece in range(1, len(X_LOADS)):
-            x_raw.append(load(f"x_raw{piece}", by_word(xT)[:, :, x_first[piece] : x_first[piece + 1]]))
-        w1_first_raw = load("w1_first_raw", by_word(w1)[:, :, :PASS])
-        w3_raw = [load("w3_raw0", by_word(w3)[:, :, :PASS])]
-        w1_cut = PASS + W1_VECTOR[1]
-        w1_vector_raw = load("w1_vector_raw", by_word(w1)[:, :, PASS:w1_cut])
-        w1_scalar_raw = load("w1_scalar_raw", by_word(w1)[:, :, w1_cut:])
-        w3_raw.append(load("w3_raw1", by_word(w3)[:, :, PASS:]))
-        parts = [slice(part * W2_PART, (part + 1) * W2_PART) for part in range(2)]
-        w2_first_raw = load("w2_first_raw", by_word(w2[:PASS, :]))
-        w2_raw = [
-            [w2_first_raw[:, :, cols] for cols in parts],
-            [load(f"w2_last_raw{part}", by_word(w2[PASS:, :])[:, :, parts[part]])[:] for part in range(2)],
+        x_rows = [load(f"x_row{j}", by_word(xT)[:, j, :]) for j in range(J)]
+        piece = PASS // 2
+        w3_first_raw = [load(f"w3_first_raw{i}", by_word(w3)[:, :, i * piece : (i + 1) * piece]) for i in range(2)]
+        w1_second_raw = [
+            load(f"w1_second_raw{i}", by_word(w1)[:, :, PASS + i * piece : PASS + (i + 1) * piece]) for i in range(2)
         ]
+        w3_raw = load("w3_raw1", by_word(w3)[:, :, PASS:])
+        w2_raw = {}
+        for part in range(2):
+            for c in range(2):
+                source = by_word(w2[c * PASS : (c + 1) * PASS, :])[:, :, part * W2_PART : (part + 1) * W2_PART]
+                if (c, part) == (1, 1):
+                    w2_raw[c, part] = tail.tile([P, J, W2_PART], F32, name="w2_raw11", offset=0, align_bytes=256)
+                    nc.sync.dma_start(out=w2_raw[c, part][:], in_=source)
+                else:
+                    w2_raw[c, part] = load(f"w2_raw{c}{part}", source)
 
-        all_q = quantised("all", T)
-        nc.gpsimd.memset(all_q[1][:], 0)
-        for piece in range(len(X_LOADS)):
-            quantise(all_q, x_first[piece], cast_plain(f"x{piece}", x_raw[piece][:], X_VECTOR[piece])[:])
+        w1_q = quantise_in("w1_0", stage_half("w1_0", w1_raw, W1_VECTOR), 1)
+
+        picked = [held([P, HALF, J], BF16, f"picked{half}") for half in range(2)]
+        columns = HALF // STRIPE
+        for j in range(J):
+            nc.vector.tensor_copy(picked[0][:, :, j], x_rows[j][:].indirect(offsets[:, :columns]))
+            nc.scalar.activation(picked[1][:, :, j], x_rows[j][:].indirect(offsets[:, columns:]), COPY)
         x_q = quantised("x", S)
-        for picked, whole in zip(x_q, all_q):
-            nc.vector.tensor_copy(picked[:], whole[:].indirect(offsets[:]))
+        for half in range(2):
+            quantise(x_q, half * HALF, picked[half][:])
 
         def first_product(weights, b, bank_number):
             bank = psum.tile([P, J, BLOCK], F32, name="bank", tag=f"bank{bank_number}")
@@ -134,86 +146,95 @@ def tile_picked_pick_glu_relu_srt_e_kernel(tc, xT, w1, w3, w2, offs, out):
                 )
             return bank[:].rearrange("p t n -> p n t")
 
-        def gate(dst, weights, b):
-            nc.scalar.activation(dst, first_product(weights, b, b), RELU)
+        def gate(dst, weights, b, bank_number):
+            nc.scalar.activation(dst, first_product(weights, b, bank_number), RELU)
 
-        def hidden(staged, gate_values, weights, b):
+        def hidden(staged, gate_values, weights, b, bank_number):
             nc.vector.tensor_tensor(
                 out=staged[:, b * BLOCK : (b + 1) * BLOCK, :],
                 in0=gate_values,
-                in1=first_product(weights, b, BLOCKS + b),
+                in1=first_product(weights, b, bank_number),
                 op=MULT,
             )
 
-        def cast_w2(c, part):
-            return cast_plain(f"w2_{c}_{part}", w2_raw[c][part], W2_VECTOR[c][part])
+        def cast_w2(c, part, vector_share):
+            return cast_plain(f"w2_{c}_{part}", w2_raw[c, part][:], vector_share)
 
         def quantise_w2(c, part, staged):
             quantise(w2_q[c], part * W2_PART, staged[:])
 
-        last = BLOCKS - 1
+        def quantise_h(first_block, blocks):
+            tokens = slice(first_block * BLOCK, (first_block + blocks) * BLOCK)
+            quantise(h_q[1], tokens.start, h_second[:, tokens, :])
 
-        w1_q = quantise_whole("w1_0", cast_dealt("w1_0", w1_first_raw, W1_VECTOR[0]))
-        w3_q = quantise_whole("w3_0", cast_dealt("w3_0", w3_raw[0], W3_VECTOR[0]))
-        for warm_up in range(2):
-            unread = psum.tile([P, S], F32, name="bank", tag="bank7")
-            multiply(unread[:], x_q, slice(0, P), x_q, slice(0, S), True, True)
-        first_gates = held([P, BLOCKS, BLOCK, J], F32, "gates0", over="w3_raw0")
-        gates = [first_gates[:, b, :, :] for b in range(BLOCKS)]
-        for b in range(BLOCKS):
-            gate(gates[b], w1_q, b)
-        w1_staged = held([P, PASS, J], BF16, "w1_1_staged")
-        dealt = w1_staged[:].rearrange("p (t m) (u e) -> p m u t e", t=J, e=2)
-        cut = W1_VECTOR[1] // J
-        nc.vector.tensor_copy(out=dealt[:, :cut], in_=w1_vector_raw[:].rearrange("p (u e) (m t) -> p m u t e", t=J, e=2))
-        nc.scalar.copy(out=dealt[:, cut:], in_=w1_scalar_raw[:].rearrange("p (u e) (m t) -> p m u t e", t=J, e=2))
-        h_first = held([P, S, J], BF16, "h_first", over="w1_vector_raw")
-        hidden(h_first, gates[0], w3_q, 0)
-        w1_q = quantise_whole("w1_1", w1_staged)
-        hidden(h_first, gates[1], w3_q, 1)
-        w3_staged = cast_dealt("w3_1", w3_raw[1], W3_VECTOR[1])
-        for b in range(2, BLOCKS):
-            hidden(h_first, gates[b], w3_q, b)
-        w3_q = quantise_whole("w3_1", w3_staged)
-        h_q = [quantised("h0", S)]
-        quantise(h_q[0], 0, h_first[:])
-
-        early_gates = held([P, last, BLOCK, J], F32, "gates1")
-        for b in range(last):
-            gate(early_gates[:, b, :, :], w1_q, b)
-        w2_q = [quantised(f"w2_{c}", N) for c in range(2)]
-        w2_staged = [cast_w2(0, part) for part in range(2)]
-        h_second = held([P, S, J], BF16, "h_second")
-        for b in range(2):
-            hidden(h_second, early_gates[:, b, :, :], w3_q, b)
-            quantise_w2(0, b, w2_staged[b])
-        h_q.append(quantised("h1", S))
-        quantise(h_q[1], 0, h_second[:, :TOKENS_OUT, :])
-        quantise_w2(1, 0, cast_w2(1, 0))
-        w2_last_staged = cast_w2(1, 1)
-        last_gate = held([P, BLOCK, J], F32, "gate1_last", over="w2_last_raw0")
-        gate(last_gate[:], w1_q, last)
-        hidden(h_second, early_gates[:, last - 1, :, :], w3_q, last - 1)
-        quantise_w2(1, 1, w2_last_staged)
-        quantise(h_q[1], (last - 1) * BLOCK, h_second[:, (last - 1) * BLOCK : last * BLOCK, :])
-        hidden(h_second, last_gate[:], w3_q, last)
-        quantise(h_q[1], last * BLOCK, h_second[:, last * BLOCK :, :])
-
-        def output(first_tile, tiles, cols, bank_number, copy):
+        def output(first_tile, tiles, cols, bank_number, copy, result):
             width = cols.stop - cols.start
             bank = psum.tile([P, tiles, width], F32, name="bank", tag=f"bank{bank_number}")
-            for i in range(tiles):
-                rows = slice((first_tile + i) * P, (first_tile + i + 1) * P)
-                for c in range(2):
-                    multiply(bank[:, i, :], w2_q[c], rows, h_q[c], cols, c == 0, c == 1)
-            result = held([P, tiles, width], F32, f"result{first_tile}_{cols.start}")
-            copy(out=result[:], in_=bank[:])
+            for c in range(2):
+                for i in range(tiles):
+                    rows = slice((first_tile + i) * P, (first_tile + i + 1) * P)
+                    multiply(bank[:, i, :], w2_q[c], rows, h_q[c], cols, (c, i) == (0, 0), (c, i) == (1, tiles - 1))
+            staged = result[:].rearrange("p (i n) -> p i n", i=tiles)
+            copy(out=staged, in_=bank[:])
             rows = slice(first_tile * P, (first_tile + tiles) * P)
-            nc.sync.dma_start(out=out[rows, cols].rearrange("(i p) n -> p i n", p=P), in_=result[:])
+            nc.sync.dma_start(out=out[rows, cols].rearrange("(i p) n -> p i n", p=P), in_=staged)
 
-        for m, bank_number in enumerate((0, 1, 2, 4)):
-            output(m, 1, slice(0, TOKENS_OUT), bank_number, nc.scalar.copy)
-        for pair, (bank_number, copy) in enumerate(((5, nc.scalar.copy), (6, nc.vector.tensor_copy))):
-            output(2 * pair, 2, slice((last - 1) * BLOCK, last * BLOCK), bank_number, copy)
-        for pair, (bank_number, copy) in enumerate(((3, nc.vector.tensor_copy), (7, nc.scalar.copy))):
-            output(2 * pair, 2, slice(last * BLOCK, S), bank_number, copy)
+        def placed(columns, name, first):
+            return tail.tile([P, columns], F32, name=name, offset=4 * first, align_bytes=256)
+
+        w3_q = quantised("w3_0", PASS)
+        run = piece // J
+        for i in range(2):
+            w3_staged = held([P, piece, J], BF16, f"w3_0_staged{i}")
+            cast_dealt(w3_staged, 0, w3_first_raw[i], W3_FIRST_VECTOR[i])
+            for t in range(J):
+                quantise(w3_q, t * P + i * run, w3_staged[:, t * run : (t + 1) * run, :])
+        gates = held([P, BLOCKS, BLOCK, J], F32, "gates0", over="w3_first_raw1")
+        for b in range(BLOCKS - 1):
+            gate(gates[:, b, :, :], w1_q, b, b)
+        w1_staged = held([P, PASS, J], BF16, "w1_1_staged")
+        cast_dealt(w1_staged, 0, w1_second_raw[0], piece)
+        cast_dealt(w1_staged, piece, w1_second_raw[1], 0)
+        h_first = held([P, S, J], BF16, "h_first", over="w1_second_raw0")
+        hidden(h_first, gates[:, 0, :, :], w3_q, 0, 3)
+        gate(gates[:, BLOCKS - 1, :, :], w1_q, BLOCKS - 1, 0)
+        for b, bank_number in ((1, 4), (2, 5), (3, 3)):
+            hidden(h_first, gates[:, b, :, :], w3_q, b, bank_number)
+        w1_q = quantise_in("w1_1", w1_staged, J)
+        w3_q = quantise_in("w3_1", stage_half("w3_1", w3_raw, W3_VECTOR), J)
+        h_q = [quantised("h0", S, over="w3_1_staged")]
+        quantise(h_q[0], 0, h_first[:])
+
+        early_gates = held([P, 2, BLOCK, J], F32, "gates1", over="w3_raw1")
+        h_second = held([P, S, J], BF16, "h_second")
+        h_q.append(quantised("h1", S))
+        w2_q = [quantised(f"w2_{c}", N) for c in range(2)]
+        for b in range(2):
+            gate(early_gates[:, b, :, :], w1_q, b, 1 + b)
+        hidden(h_second, early_gates[:, 0, :, :], w3_q, 0, 4)
+        lower_staged = [cast_w2(0, 0, W2_PART), cast_w2(1, 0, 0)]
+        hidden(h_second, early_gates[:, 1, :, :], w3_q, 1, 5)
+        for c in range(2):
+            quantise_w2(c, 0, lower_staged[c])
+        quantise_h(0, 2)
+        third_gate = held([P, BLOCK, J], F32, "gate1_third", over="w2_raw10")
+        gate(third_gate[:], w1_q, 2, 1)
+        hidden(h_second, third_gate[:], w3_q, 2, 4)
+        quantise_w2(0, 1, cast_w2(0, 1, 0))
+        last_staged = cast_w2(1, 1, W2_LAST_VECTOR)
+        quantise_h(2, 1)
+        quantise_w2(1, 1, last_staged)
+        last_gate = placed(BLOCK * J, "gate1_last", 0)[:].rearrange("p (n t) -> p n t", t=J)
+        gate(last_gate, w1_q, 3, 2)
+        hidden(h_second, last_gate, w3_q, 3, 5)
+
+        first, third, fourth = slice(0, HALF), slice(2 * BLOCK, 3 * BLOCK), slice(3 * BLOCK, S)
+        output(0, 1, first, 0, nc.scalar.copy, placed(HALF, "result0", 2 * HALF))
+        output(1, 1, first, 3, nc.scalar.copy, placed(HALF, "result1", 3 * HALF))
+        output(0, 2, third, 6, nc.vector.tensor_copy, placed(HALF, "result2", 0))
+        quantise_h(3, 1)
+        output(2, 1, first, 7, nc.scalar.copy, held([P, HALF], F32, "result3"))
+        output(3, 1, first, 1, nc.scalar.copy, held([P, HALF], F32, "result4"))
+        output(2, 2, third, 4, nc.vector.tensor_copy, placed(HALF, "result5", HALF))
+        output(0, 2, fourth, 2, nc.vector.tensor_copy, held([P, HALF], F32, "result6"))
+        output(2, 2, fourth, 0, nc.scalar.copy, held([P, HALF], F32, "result7"))

@@ -28,7 +28,7 @@ STRIPE = 16
 W1_VECTOR = 336
 W3_FIRST_VECTOR = (80, 128)
 W3_VECTOR = 224
-W2_LAST_VECTOR = 96
+W2_FIRST_VECTOR = 224
 
 
 def tile_picked_pick_glu_relu_srt_e_kernel(tc, xT, w1, w3, w2, offs, out):
@@ -195,7 +195,7 @@ def tile_picked_pick_glu_relu_srt_e_kernel(tc, xT, w1, w3, w2, offs, out):
         w1_staged = held([P, PASS, J], BF16, "w1_1_staged")
         cast_dealt(w1_staged, 0, w1_second_raw[0], piece)
         cast_dealt(w1_staged, piece, w1_second_raw[1], 0)
-        h_first = held([P, S, J], BF16, "h_first", over="w1_second_raw0")
+        h_first = held([P, S, J], BF16, "h_first")
         hidden(h_first, gates[:, 0, :, :], w3_q, 0, 3)
         gate(gates[:, BLOCKS - 1, :, :], w1_q, BLOCKS - 1, 0)
         for b, bank_number in ((1, 4), (2, 5), (3, 3)):
@@ -212,7 +212,7 @@ def tile_picked_pick_glu_relu_srt_e_kernel(tc, xT, w1, w3, w2, offs, out):
         for b in range(2):
             gate(early_gates[:, b, :, :], w1_q, b, 1 + b)
         hidden(h_second, early_gates[:, 0, :, :], w3_q, 0, 4)
-        lower_staged = [cast_w2(0, 0, W2_PART), cast_w2(1, 0, 0)]
+        lower_staged = [cast_w2(0, 0, W2_FIRST_VECTOR), cast_w2(1, 0, 0)]
         hidden(h_second, early_gates[:, 1, :, :], w3_q, 1, 5)
         for c in range(2):
             quantise_w2(c, 0, lower_staged[c])
@@ -221,20 +221,21 @@ def tile_picked_pick_glu_relu_srt_e_kernel(tc, xT, w1, w3, w2, offs, out):
         gate(third_gate[:], w1_q, 2, 1)
         hidden(h_second, third_gate[:], w3_q, 2, 4)
         quantise_w2(0, 1, cast_w2(0, 1, 0))
-        last_staged = cast_w2(1, 1, W2_LAST_VECTOR)
         quantise_h(2, 1)
-        quantise_w2(1, 1, last_staged)
-        last_gate = placed(BLOCK * J, "gate1_last", 0)[:].rearrange("p (n t) -> p n t", t=J)
+        last_gate = held([P, BLOCK * J], F32, "gate1_last", over="w2_raw01")[:].rearrange("p (n t) -> p n t", t=J)
         gate(last_gate, w1_q, 3, 2)
         hidden(h_second, last_gate, w3_q, 3, 5)
-
-        first, third, fourth = slice(0, HALF), slice(2 * BLOCK, 3 * BLOCK), slice(3 * BLOCK, S)
-        output(0, 1, first, 0, nc.scalar.copy, placed(HALF, "result0", 2 * HALF))
-        output(1, 1, first, 3, nc.scalar.copy, placed(HALF, "result1", 3 * HALF))
-        output(0, 2, third, 6, nc.vector.tensor_copy, placed(HALF, "result2", 0))
+        first, second = slice(0, HALF), slice(HALF, S)
+        third, fourth = slice(2 * BLOCK, 3 * BLOCK), slice(3 * BLOCK, S)
+        quantise(w2_q[1], 2 * P, cast_plain("w2_last0", w2_raw[1, 1][:, :, :P], 0)[:])
         quantise_h(3, 1)
+        output(0, 1, first, 0, nc.scalar.copy, held([P, HALF], F32, "result0"))
+        quantise(w2_q[1], 3 * P, cast_plain("w2_last1", w2_raw[1, 1][:, :, P:], 0)[:])
+
+        output(1, 1, first, 3, nc.scalar.copy, held([P, HALF], F32, "result1"))
+        output(0, 2, third, 6, nc.vector.tensor_copy, held([P, HALF], F32, "result2", over="w2_raw01"))
         output(2, 1, first, 7, nc.scalar.copy, held([P, HALF], F32, "result3"))
-        output(3, 1, first, 1, nc.scalar.copy, held([P, HALF], F32, "result4"))
-        output(2, 2, third, 4, nc.vector.tensor_copy, placed(HALF, "result5", HALF))
-        output(0, 2, fourth, 2, nc.vector.tensor_copy, held([P, HALF], F32, "result6"))
-        output(2, 2, fourth, 0, nc.scalar.copy, held([P, HALF], F32, "result7"))
+        output(0, 2, fourth, 4, nc.vector.tensor_copy, held([P, HALF], F32, "result4"))
+        output(2, 1, second, 2, nc.scalar.copy, held([P, HALF], F32, "result5"))
+        output(3, 1, first, 1, nc.vector.tensor_copy, held([P, HALF], F32, "result6"))
+        output(3, 1, second, 5, nc.scalar.copy, held([P, HALF], F32, "result7"))

@@ -26,9 +26,9 @@ LINE = 4
 STRIPE = 16
 
 W1_VECTOR = 336
-W3_FIRST_VECTOR = (80, 128)
-W3_VECTOR = 224
-W2_FIRST_VECTOR = 224
+W1_EARLY = 288
+W3_FIRST_VECTOR = (96, 144)
+W3_VECTOR = 192
 
 
 def tile_picked_pick_glu_relu_srt_e_kernel(tc, xT, w1, w3, w2, offs, out):
@@ -36,7 +36,7 @@ def tile_picked_pick_glu_relu_srt_e_kernel(tc, xT, w1, w3, w2, offs, out):
 
     with ExitStack() as ctx:
         keep = ctx.enter_context(tc.tile_pool(name="keep", bufs=1))
-        tail = ctx.enter_context(tc.tile_pool(name="tail", bufs=1))
+        shared = ctx.enter_context(tc.tile_pool(name="shared", bufs=1))
         psum = ctx.enter_context(tc.psum_pool(name="psum", bufs=1))
 
         def held(shape, dtype, name, over=None):
@@ -57,8 +57,11 @@ def tile_picked_pick_glu_relu_srt_e_kernel(tc, xT, w1, w3, w2, offs, out):
             if cut < dst.shape[1]:
                 nc.scalar.copy(out=dst[:, cut:], in_=src[:, cut:])
 
-        def quantised(name, width, over=None):
-            return held([P, width], U32, name + "_codes", over), held([P, width], U8, name + "_scales")
+        def placed(shape, dtype, name, first_byte):
+            return shared.tile(shape, dtype, name=name, offset=first_byte, align_bytes=256)
+
+        def quantised(name, width):
+            return held([P, width], U32, name + "_codes"), held([P, width], U8, name + "_scales")
 
         def quantise(operand, first, staged):
             codes, scales = operand
@@ -113,19 +116,16 @@ def tile_picked_pick_glu_relu_srt_e_kernel(tc, xT, w1, w3, w2, offs, out):
         x_rows = [load(f"x_row{j}", by_word(xT)[:, j, :]) for j in range(J)]
         piece = PASS // 2
         w3_first_raw = [load(f"w3_first_raw{i}", by_word(w3)[:, :, i * piece : (i + 1) * piece]) for i in range(2)]
-        w1_second_raw = [
-            load(f"w1_second_raw{i}", by_word(w1)[:, :, PASS + i * piece : PASS + (i + 1) * piece]) for i in range(2)
-        ]
-        w3_raw = load("w3_raw1", by_word(w3)[:, :, PASS:])
+        w1_early_raw = load("w1_early_raw", by_word(w1)[:, :, PASS : PASS + W1_EARLY])
+        w1_late_raw = load("w1_late_raw", by_word(w1)[:, :, PASS + W1_EARLY :])
+        w3_early_raw = load("w3_early_raw", by_word(w3)[:, :, PASS : PASS + piece])
+        w3_late_raw = placed([P, J, piece], F32, "w3_late_raw", 0)
+        nc.sync.dma_start(out=w3_late_raw[:], in_=by_word(w3)[:, :, PASS + piece :])
         w2_raw = {}
         for part in range(2):
             for c in range(2):
                 source = by_word(w2[c * PASS : (c + 1) * PASS, :])[:, :, part * W2_PART : (part + 1) * W2_PART]
-                if (c, part) == (1, 1):
-                    w2_raw[c, part] = tail.tile([P, J, W2_PART], F32, name="w2_raw11", offset=0, align_bytes=256)
-                    nc.sync.dma_start(out=w2_raw[c, part][:], in_=source)
-                else:
-                    w2_raw[c, part] = load(f"w2_raw{c}{part}", source)
+                w2_raw[c, part] = load(f"w2_raw{c}{part}", source)
 
         w1_q = quantise_in("w1_0", stage_half("w1_0", w1_raw, W1_VECTOR), 1)
 
@@ -165,22 +165,21 @@ def tile_picked_pick_glu_relu_srt_e_kernel(tc, xT, w1, w3, w2, offs, out):
 
         def quantise_h(first_block, blocks):
             tokens = slice(first_block * BLOCK, (first_block + blocks) * BLOCK)
-            quantise(h_q[1], tokens.start, h_second[:, tokens, :])
+            quantise(h_second_q, tokens.start, h_second[:, tokens, :])
 
         def output(first_tile, tiles, cols, bank_number, copy, result):
             width = cols.stop - cols.start
             bank = psum.tile([P, tiles, width], F32, name="bank", tag=f"bank{bank_number}")
+            half, start = divmod(cols.start, HALF)
+            moving = ((h_first_q[half], slice(start, start + width)), (h_second_q, cols))
             for c in range(2):
                 for i in range(tiles):
                     rows = slice((first_tile + i) * P, (first_tile + i + 1) * P)
-                    multiply(bank[:, i, :], w2_q[c], rows, h_q[c], cols, (c, i) == (0, 0), (c, i) == (1, tiles - 1))
+                    multiply(bank[:, i, :], w2_q[c], rows, *moving[c], (c, i) == (0, 0), (c, i) == (1, tiles - 1))
             staged = result[:].rearrange("p (i n) -> p i n", i=tiles)
             copy(out=staged, in_=bank[:])
             rows = slice(first_tile * P, (first_tile + tiles) * P)
             nc.sync.dma_start(out=out[rows, cols].rearrange("(i p) n -> p i n", p=P), in_=staged)
-
-        def placed(columns, name, first):
-            return tail.tile([P, columns], F32, name=name, offset=4 * first, align_bytes=256)
 
         w3_q = quantised("w3_0", PASS)
         run = piece // J
@@ -193,49 +192,52 @@ def tile_picked_pick_glu_relu_srt_e_kernel(tc, xT, w1, w3, w2, offs, out):
         for b in range(BLOCKS - 1):
             gate(gates[:, b, :, :], w1_q, b, b)
         w1_staged = held([P, PASS, J], BF16, "w1_1_staged")
-        cast_dealt(w1_staged, 0, w1_second_raw[0], piece)
-        cast_dealt(w1_staged, piece, w1_second_raw[1], 0)
+        cast_dealt(w1_staged, 0, w1_early_raw, W1_EARLY)
+        cast_dealt(w1_staged, W1_EARLY, w1_late_raw, 0)
         h_first = held([P, S, J], BF16, "h_first")
         hidden(h_first, gates[:, 0, :, :], w3_q, 0, 3)
         gate(gates[:, BLOCKS - 1, :, :], w1_q, BLOCKS - 1, 0)
         for b, bank_number in ((1, 4), (2, 5), (3, 3)):
             hidden(h_first, gates[:, b, :, :], w3_q, b, bank_number)
         w1_q = quantise_in("w1_1", w1_staged, J)
-        w3_q = quantise_in("w3_1", stage_half("w3_1", w3_raw, W3_VECTOR), J)
-        h_q = [quantised("h0", S, over="w3_1_staged")]
-        quantise(h_q[0], 0, h_first[:])
+        w3_staged = held([P, PASS, J], BF16, "w3_1_staged")
+        cast_dealt(w3_staged, 0, w3_early_raw, W3_VECTOR)
+        cast_dealt(w3_staged, piece, w3_late_raw, 0)
+        h_first_q = [
+            quantised("h0_lower", HALF),
+            (placed([P, HALF], U32, "h0_upper_codes", 0), held([P, HALF], U8, "h0_upper_scales")),
+        ]
+        quantise(h_first_q[0], 0, h_first[:, :HALF, :])
+        w3_q = quantise_in("w3_1", w3_staged, J)
+        quantise(h_first_q[1], 0, h_first[:, HALF:, :])
 
-        early_gates = held([P, 2, BLOCK, J], F32, "gates1", over="w3_raw1")
+        early_gates = placed([P, 3, BLOCK, J], F32, "gates1", HALF * 4)
         h_second = held([P, S, J], BF16, "h_second")
-        h_q.append(quantised("h1", S))
+        h_second_q = quantised("h1", S)
         w2_q = [quantised(f"w2_{c}", N) for c in range(2)]
-        for b in range(2):
-            gate(early_gates[:, b, :, :], w1_q, b, 1 + b)
-        hidden(h_second, early_gates[:, 0, :, :], w3_q, 0, 4)
-        lower_staged = [cast_w2(0, 0, W2_FIRST_VECTOR), cast_w2(1, 0, 0)]
-        hidden(h_second, early_gates[:, 1, :, :], w3_q, 1, 5)
-        for c in range(2):
-            quantise_w2(c, 0, lower_staged[c])
+        for b, bank_number in enumerate((1, 2, 0)):
+            gate(early_gates[:, b, :, :], w1_q, b, bank_number)
+        first_staged = cast_w2(0, 0, W2_PART)
+        for b, bank_number in enumerate((4, 5, 3)):
+            hidden(h_second, early_gates[:, b, :, :], w3_q, b, bank_number)
+        quantise_w2(1, 0, cast_w2(1, 0, 0))
+        quantise_w2(0, 0, first_staged)
         quantise_h(0, 2)
-        third_gate = held([P, BLOCK, J], F32, "gate1_third", over="w2_raw10")
-        gate(third_gate[:], w1_q, 2, 1)
-        hidden(h_second, third_gate[:], w3_q, 2, 4)
-        quantise_w2(0, 1, cast_w2(0, 1, 0))
         quantise_h(2, 1)
-        last_gate = held([P, BLOCK * J], F32, "gate1_last", over="w2_raw01")[:].rearrange("p (n t) -> p n t", t=J)
-        gate(last_gate, w1_q, 3, 2)
-        hidden(h_second, last_gate, w3_q, 3, 5)
-        first, second = slice(0, HALF), slice(HALF, S)
-        third, fourth = slice(2 * BLOCK, 3 * BLOCK), slice(3 * BLOCK, S)
-        quantise(w2_q[1], 2 * P, cast_plain("w2_last0", w2_raw[1, 1][:, :, :P], 0)[:])
-        quantise_h(3, 1)
-        output(0, 1, first, 0, nc.scalar.copy, held([P, HALF], F32, "result0"))
+        third_staged = cast_plain("w2_last0", w2_raw[1, 1][:, :, :P], P)
+        quantise_w2(0, 1, cast_w2(0, 1, 0))
+        quantise(w2_q[1], 2 * P, third_staged[:])
+        last_gate = held([P, BLOCK * J], F32, "gate1_last", over="w2_1_0_staged")[:].rearrange("p (n t) -> p n t", t=J)
+        gate(last_gate, w1_q, 3, 1)
+        hidden(h_second, last_gate, w3_q, 3, 4)
         quantise(w2_q[1], 3 * P, cast_plain("w2_last1", w2_raw[1, 1][:, :, P:], 0)[:])
+        quantise_h(3, 1)
 
-        output(1, 1, first, 3, nc.scalar.copy, held([P, HALF], F32, "result1"))
-        output(0, 2, third, 6, nc.vector.tensor_copy, held([P, HALF], F32, "result2", over="w2_raw01"))
-        output(2, 1, first, 7, nc.scalar.copy, held([P, HALF], F32, "result3"))
-        output(0, 2, fourth, 4, nc.vector.tensor_copy, held([P, HALF], F32, "result4"))
-        output(2, 1, second, 2, nc.scalar.copy, held([P, HALF], F32, "result5"))
-        output(3, 1, first, 1, nc.vector.tensor_copy, held([P, HALF], F32, "result6"))
-        output(3, 1, second, 5, nc.scalar.copy, held([P, HALF], F32, "result7"))
+        first = slice(0, HALF)
+        third, fourth = slice(2 * BLOCK, 3 * BLOCK), slice(3 * BLOCK, S)
+        for m, bank_number in enumerate((6, 7, 0)):
+            output(m, 1, first, bank_number, nc.scalar.copy, held([P, HALF], F32, f"result{m}"))
+        output(0, 3, third, 2, nc.vector.tensor_copy, held([P, 3 * BLOCK], F32, "result3", over="w2_1_0_staged"))
+        output(3, 1, first, 3, nc.scalar.copy, held([P, HALF], F32, "result4"))
+        output(0, 3, fourth, 5, nc.vector.tensor_copy, held([P, 3 * BLOCK], F32, "result5"))
+        output(3, 1, slice(HALF, S), 1, nc.scalar.copy, held([P, HALF], F32, "result6"))

from contextlib import ExitStack

import concourse.mybir as mybir

K, T, S, H, N = 512, 1024, 512, 1024, 512
FLOPS = 2 * S * (2 * K * H + H * N)

F32 = mybir.dt.float32
BF16 = mybir.dt.bfloat16
U32 = mybir.dt.uint32
U16 = mybir.dt.uint16
U8 = mybir.dt.uint8
FP8X4 = mybir.dt.float8_e4m3fn_x4
MULT = mybir.AluOpType.mult
RELU = mybir.ActivationFunctionType.Relu
COPY = mybir.ActivationFunctionType.Copy

P = 128
J = 4
PASS = P * J
BLOCK = 128
BLOCKS = S // BLOCK
HALF = S // 2
W2_PART = N // 2
LINE = 4
STRIPE = 16

W1_VECTOR = 336
W1_EARLY = 288
W3_FIRST_VECTOR = (96, 144)
W3_VECTOR = 192


def tile_picked_pick_glu_relu_srt_e_kernel(tc, xT, w1, w3, w2, offs, out):
    nc = tc.nc

    with ExitStack() as ctx:
        keep = ctx.enter_context(tc.tile_pool(name="keep", bufs=1))
        shared = ctx.enter_context(tc.tile_pool(name="shared", bufs=1))
        psum = ctx.enter_context(tc.psum_pool(name="psum", bufs=1))

        def held(shape, dtype, name, over=None):
            return keep.tile(shape, dtype, name=name, tag=over or name, align_bytes=256)

        def load(name, source):
            raw = held(list(source.shape), F32, name)
            nc.sync.dma_start(out=raw[:], in_=source)
            return raw

        def by_word(matrix):
            return matrix.rearrange("(p j) w -> p j w", j=J)

        def shared_cast(dst, src, vector_share):
            cut = vector_share // LINE
            if cut > 0:
                nc.vector.tensor_copy(out=dst[:, :cut], in_=src[:, :cut])
            if cut < dst.shape[1]:
                nc.scalar.copy(out=dst[:, cut:], in_=src[:, cut:])

        def placed(shape, dtype, name, first_byte):
            return shared.tile(shape, dtype, name=name, offset=first_byte, align_bytes=256)

        def quantised(name, width):
            return held([P, width], U32, name + "_codes"), held([P, width], U8, name + "_scales")

        def quantise(operand, first, staged):
            codes, scales = operand
            cols = slice(first, first + staged.shape[1])
            nc.vector.quantize_mx(
                out=codes[:, cols].bitcast(FP8X4), scales=scales[:, cols], in_=staged.rearrange("p w j -> p (w j)")
            )

        def multiply(dst, stationary, rows, moving, cols, start, stop):
            nc.tensor.matmul_mx(
                out=dst,
                lhsT=stationary[0][:, rows].bitcast(FP8X4),
                lhsT_scale=stationary[1][:, rows],
                rhs=moving[0][:, cols].bitcast(FP8X4),
                rhs_scale=moving[1][:, cols],
                start=start,
                stop=stop,
            )

        def cast_plain(name, raw, vector_share):
            staged = held([P, raw.shape[2], J], BF16, name + "_staged")
            shared_cast(
                staged[:].rearrange("p (g i) (u e) -> p g u i e", i=LINE, e=2),
                raw.rearrange("p (u e) (g i) -> p g u i e", i=LINE, e=2),
                vector_share,
            )
            return staged

        def cast_dealt(staged, first, raw, vector_share):
            groups = slice(first // J, (first + raw.shape[2]) // J)
            shared_cast(
                staged[:].rearrange("p (t m) (u e) -> p m u t e", t=J, e=2)[:, groups],
                raw[:].rearrange("p (u e) (m t) -> p m u t e", t=J, e=2),
                vector_share,
            )

        def stage_half(name, raw, vector_share):
            staged = held([P, PASS, J], BF16, name + "_staged")
            cast_dealt(staged, 0, raw, vector_share)
            return staged

        def quantise_in(name, staged, pieces):
            operand = quantised(name, PASS)
            width = PASS // pieces
            for piece in range(pieces):
                quantise(operand, piece * width, staged[:, piece * width : (piece + 1) * width, :])
            return operand

        w1_raw = load("w1_raw0", by_word(w1)[:, :, :PASS])
        offsets = keep.tile([P, S // STRIPE], U16, name="offsets")
        nc.sync.dma_start(offsets[:], offs)
        x_rows = [load(f"x_row{j}", by_word(xT)[:, j, :]) for j in range(J)]
        piece = PASS // 2
        w3_first_raw = [load(f"w3_first_raw{i}", by_word(w3)[:, :, i * piece : (i + 1) * piece]) for i in range(2)]
        w1_early_raw = load("w1_early_raw", by_word(w1)[:, :, PASS : PASS + W1_EARLY])
        w1_late_raw = load("w1_late_raw", by_word(w1)[:, :, PASS + W1_EARLY :])
        w3_early_raw = load("w3_early_raw", by_word(w3)[:, :, PASS : PASS + piece])
        w3_late_raw = placed([P, J, piece], F32, "w3_late_raw", 0)
        nc.sync.dma_start(out=w3_late_raw[:], in_=by_word(w3)[:, :, PASS + piece :])
        w2_raw = {}
        for part in range(2):
            for c in range(2):
                source = by_word(w2[c * PASS : (c + 1) * PASS, :])[:, :, part * W2_PART : (part + 1) * W2_PART]
                w2_raw[c, part] = load(f"w2_raw{c}{part}", source)

        w1_q = quantise_in("w1_0", stage_half("w1_0", w1_raw, W1_VECTOR), 1)

        picked = [held([P, HALF, J], BF16, f"picked{half}") for half in range(2)]
        columns = HALF // STRIPE
        for j in range(J):
            nc.vector.tensor_copy(picked[0][:, :, j], x_rows[j][:].indirect(offsets[:, :columns]))
            nc.scalar.activation(picked[1][:, :, j], x_rows[j][:].indirect(offsets[:, columns:]), COPY)
        x_q = quantised("x", S)
        for half in range(2):
            quantise(x_q, half * HALF, picked[half][:])

        def first_product(weights, b, bank_number):
            bank = psum.tile([P, J, BLOCK], F32, name="bank", tag=f"bank{bank_number}")
            for t in range(J):
                multiply(
                    bank[:, t, :], weights, slice(t * P, (t + 1) * P), x_q, slice(b * BLOCK, (b + 1) * BLOCK), True, True
                )
            return bank[:].rearrange("p t n -> p n t")

        def gate(dst, weights, b, bank_number):
            nc.scalar.activation(dst, first_product(weights, b, bank_number), RELU)

        def hidden(staged, gate_values, weights, b, bank_number):
            nc.vector.tensor_tensor(
                out=staged[:, b * BLOCK : (b + 1) * BLOCK, :],
                in0=gate_values,
                in1=first_product(weights, b, bank_number),
                op=MULT,
            )

        def cast_w2(c, part, vector_share):
            return cast_plain(f"w2_{c}_{part}", w2_raw[c, part][:], vector_share)

        def quantise_w2(c, part, staged):
            quantise(w2_q[c], part * W2_PART, staged[:])

        def quantise_h(first_block, blocks):
            tokens = slice(first_block * BLOCK, (first_block + blocks) * BLOCK)
            quantise(h_second_q, tokens.start, h_second[:, tokens, :])

        def output(first_tile, tiles, cols, bank_number, copy, result):
            width = cols.stop - cols.start
            bank = psum.tile([P, tiles, width], F32, name="bank", tag=f"bank{bank_number}")
            half, start = divmod(cols.start, HALF)
            moving = ((h_first_q[half], slice(start, start + width)), (h_second_q, cols))
            for c in range(2):
                for i in range(tiles):
                    rows = slice((first_tile + i) * P, (first_tile + i + 1) * P)
                    multiply(bank[:, i, :], w2_q[c], rows, *moving[c], (c, i) == (0, 0), (c, i) == (1, tiles - 1))
            staged = result[:].rearrange("p (i n) -> p i n", i=tiles)
            copy(out=staged, in_=bank[:])
            rows = slice(first_tile * P, (first_tile + tiles) * P)
            nc.sync.dma_start(out=out[rows, cols].rearrange("(i p) n -> p i n", p=P), in_=staged)

        w3_q = quantised("w3_0", PASS)
        run = piece // J
        for i in range(2):
            w3_staged = held([P, piece, J], BF16, f"w3_0_staged{i}")
            cast_dealt(w3_staged, 0, w3_first_raw[i], W3_FIRST_VECTOR[i])
            for t in range(J):
                quantise(w3_q, t * P + i * run, w3_staged[:, t * run : (t + 1) * run, :])
        gates = held([P, BLOCKS, BLOCK, J], F32, "gates0", over="w3_first_raw1")
        for b in range(BLOCKS - 1):
            gate(gates[:, b, :, :], w1_q, b, b)
        w1_staged = held([P, PASS, J], BF16, "w1_1_staged")
        cast_dealt(w1_staged, 0, w1_early_raw, W1_EARLY)
        cast_dealt(w1_staged, W1_EARLY, w1_late_raw, 0)
        h_first = held([P, S, J], BF16, "h_first")
        hidden(h_first, gates[:, 0, :, :], w3_q, 0, 3)
        gate(gates[:, BLOCKS - 1, :, :], w1_q, BLOCKS - 1, 0)
        for b, bank_number in ((1, 4), (2, 5), (3, 3)):
            hidden(h_first, gates[:, b, :, :], w3_q, b, bank_number)
        w1_q = quantise_in("w1_1", w1_staged, J)
        w3_staged = held([P, PASS, J], BF16, "w3_1_staged")
        cast_dealt(w3_staged, 0, w3_early_raw, W3_VECTOR)
        cast_dealt(w3_staged, piece, w3_late_raw, 0)
        h_first_q = [
            quantised("h0_lower", HALF),
            (placed([P, HALF], U32, "h0_upper_codes", 0), held([P, HALF], U8, "h0_upper_scales")),
        ]
        quantise(h_first_q[0], 0, h_first[:, :HALF, :])
        w3_q = quantise_in("w3_1", w3_staged, J)
        quantise(h_first_q[1], 0, h_first[:, HALF:, :])

        early_gates = placed([P, 3, BLOCK, J], F32, "gates1", HALF * 4)
        h_second = held([P, S, J], BF16, "h_second")
        h_second_q = quantised("h1", S)
        w2_q = [quantised(f"w2_{c}", N) for c in range(2)]
        for b, bank_number in enumerate((1, 2, 0)):
            gate(early_gates[:, b, :, :], w1_q, b, bank_number)
        first_staged = cast_w2(0, 0, W2_PART)
        for b, bank_number in enumerate((4, 5, 3)):
            hidden(h_second, early_gates[:, b, :, :], w3_q, b, bank_number)
        quantise_w2(1, 0, cast_w2(1, 0, 0))
        quantise_w2(0, 0, first_staged)
        quantise_h(0, 2)
        quantise_h(2, 1)
        third_staged = cast_plain("w2_last0", w2_raw[1, 1][:, :, :P], P)
        quantise_w2(0, 1, cast_w2(0, 1, 0))
        quantise(w2_q[1], 2 * P, third_staged[:])
        last_gate = held([P, BLOCK * J], F32, "gate1_last", over="w2_1_0_staged")[:].rearrange("p (n t) -> p n t", t=J)
        gate(last_gate, w1_q, 3, 1)
        hidden(h_second, last_gate, w3_q, 3, 4)
        quantise(w2_q[1], 3 * P, cast_plain("w2_last1", w2_raw[1, 1][:, :, P:], 0)[:])
        quantise_h(3, 1)

        first = slice(0, HALF)
        third, fourth = slice(2 * BLOCK, 3 * BLOCK), slice(3 * BLOCK, S)
        for m, bank_number in enumerate((6, 7, 0)):
            output(m, 1, first, bank_number, nc.scalar.copy, held([P, HALF], F32, f"result{m}"))
        output(0, 3, third, 2, nc.vector.tensor_copy, held([P, 3 * BLOCK], F32, "result3", over="w2_1_0_staged"))
        output(3, 1, first, 3, nc.scalar.copy, held([P, HALF], F32, "result4"))
        output(0, 3, fourth, 5, nc.vector.tensor_copy, held([P, 3 * BLOCK], F32, "result5"))
        output(3, 1, slice(HALF, S), 1, nc.scalar.copy, held([P, HALF], F32, "result6"))
